import numpy as np
import ml_dtypes


def mxq(x, axis, fmt="e4m3"):
    dtype, down = {"e4m3": (ml_dtypes.float8_e4m3fn, 7), "e5m2": (ml_dtypes.float8_e5m2, 14)}[fmt]
    v = np.moveaxis(np.asarray(x, np.float32).astype(ml_dtypes.bfloat16).astype(np.float64), axis, -1)
    blocks = v.reshape(v.shape[:-1] + (-1, 32))
    amax = np.abs(blocks).max(-1, keepdims=True)
    byte = np.maximum(np.where(amax > 0, np.frexp(amax)[1] - 1 + 127, 0) - down, 1)
    scale = np.exp2(byte - 127.0)
    codes = (blocks / scale).astype(np.float32).astype(dtype).astype(np.float64)
    return np.moveaxis((codes * scale).reshape(v.shape), -1, axis)


WIDE = False


def mx_kscale(k):
    if not WIDE:
        return np.ones(k)
    levels = np.array([10, -10, 5, -5, 0])
    if k % 512:
        return np.exp2(np.random.permutation(np.resize(levels, k // 32))).repeat(32)
    a = np.empty((k // 512, 16))
    for p in range(k // 512):
        a[p, :8] = np.random.permutation(np.resize(levels, 8))
        for g in range(8):
            far = levels[np.abs(levels - a[p, g]) >= 10]
            a[p, g + 8] = far[np.random.randint(len(far))]
    return np.exp2(a.ravel()).repeat(32)


def f64(x):
    return np.asarray(x).astype(np.float64)


def striped(idx):
    return np.tile(idx.reshape(-1, 16).T, (8, 1)).astype(np.uint16)


def unstriped(offs):
    return offs[:16].T.reshape(-1).astype(np.int64)


E2M1 = np.array([0.0, 0.5, 1.0, 1.5, 2.0, 3.0, 4.0, 6.0, -0.0, -0.5, -1.0, -1.5, -2.0, -3.0, -4.0, -6.0])


def pack_weight(w, fmt):
    k, n = w.shape
    w = f64(np.asarray(w, np.float32).astype(ml_dtypes.bfloat16)).reshape(k // 32, 32, n)
    amax = np.abs(w).max(1)
    if fmt == "e4m3":
        byte = np.frexp(amax)[1] - 1 + 127 - 7
    else:
        mant, ex = np.frexp(amax / 6.0)
        byte = np.where(mant > 0.5, ex, ex - 1) + 127
    byte = np.clip(np.where(amax > 0, byte, 1), 1, 254)
    scaled = (w * np.exp2(127.0 - byte)[:, None, :]).reshape(k, n).astype(np.float32)
    by_word = np.ascontiguousarray(scaled.reshape(k // 512, 128, 4, n).transpose(0, 1, 3, 2))
    if fmt == "e4m3":
        words = by_word.astype(ml_dtypes.float8_e4m3fn).view(np.uint8)
    else:
        c = by_word.astype(ml_dtypes.float4_e2m1fn).view(np.uint8) & 0xF
        words = (c[..., 0::2] | (c[..., 1::2] << 4)).reshape(k // 512, 128, 2 * n)
    return np.ascontiguousarray(words), np.ascontiguousarray(byte.astype(np.uint8).reshape(k // 512, 16, n))


def unpack_weight(words, scales, fmt):
    g, _, n = scales.shape
    words = np.ascontiguousarray(words).reshape(g, 128, n, -1)
    if fmt == "e4m3":
        vals = words.view(ml_dtypes.float8_e4m3fn).astype(np.float64)
    else:
        nib = np.empty((g, 128, n, 4), np.uint8)
        nib[..., 0::2] = words & 0xF
        nib[..., 1::2] = words >> 4
        vals = E2M1[nib]
    vals = vals * np.repeat(np.exp2(scales.astype(np.float64) - 127.0), 8, axis=1)[..., None]
    return vals.transpose(0, 1, 3, 2).reshape(g * 512, n)


def gelu(v):
    return 0.5 * v * (1.0 + np.tanh(np.sqrt(2.0 / np.pi) * (v + 0.044715 * v**3)))


def striped8(idx):
    return np.concatenate([v.reshape(-1, 16).T for v in idx]).astype(np.uint16)


def unstriped8(offs):
    return np.stack([offs[16 * g:16 * g + 16].T.reshape(-1) for g in range(8)]).astype(np.int64)


def heads(h, wgt, idx8):
    r = np.arange(h.shape[0])
    return wgt[r // 4 % 128] * h[r[:, None], idx8[r % 512 // 64]]


K, T, S, P, K2, H, N = 1024, 2048, 1024, 512, 512, 1024, 768

def setup_inputs():
    n = np.random.standard_normal
    s = mx_kscale(K)[:, None]
    s2 = mx_kscale(K2)[:, None]
    u = mx_kscale(H)[:, None]
    tab_words, tab_scales = pack_weight(n((K, T)) * s, "e4m3")
    wt_words, wt_scales = pack_weight(n((K2, H)) / np.sqrt(K2) / s2, "e2m1")
    wo_words, wo_scales = pack_weight(n((H, N)) / np.sqrt(H) / u, "e4m3")
    return {
        "tab_words": tab_words, "tab_scales": tab_scales,
        "offs": striped(np.random.permutation(T)[:S]),
        "offs2": striped8(np.stack([np.random.permutation(S)[:P] for _ in range(8)])),
        "w1": (n((K, H)) / np.sqrt(K) / s).astype(np.float32),
        "wgt": np.repeat(np.random.uniform(0.5, 2.0, (8, P)), 16, axis=0).astype(np.float32),
        "tgt": (n((K2, P)) * s2).astype(np.float32),
        "wt_words": wt_words, "wt_scales": wt_scales,
        "slope": (-0.4 * np.exp(0.4 * n(H))).astype(np.float32),
        "gain": (np.exp(0.4 * n(H)) * u[:, 0]).astype(np.float32),
        "wo_words": wo_words, "wo_scales": wo_scales,
    }

def reference(tab_words, tab_scales, offs, offs2, w1, wgt, tgt, wt_words, wt_scales,
              slope, gain, wo_words, wo_scales):
    v = unpack_weight(tab_words, tab_scales, "e4m3")[:, unstriped(offs)]
    h = mxq(f64(w1), 0, "e4m3").T @ v
    x = heads(h, f64(wgt), unstriped8(offs2))
    wt = unpack_weight(wt_words, wt_scales, "e2m1")
    b = wt.T @ mxq(f64(tgt), 0, "e4m3")
    d = x - b
    z = np.exp(f64(slope)[:, None] * np.square(d)) * f64(gain)[:, None]
    wo = unpack_weight(wo_words, wo_scales, "e4m3")
    return wo.T @ mxq(z, 0, "e4m3")

@@ -1,0 +1,267 @@
+from contextlib import ExitStack
+
+import concourse.mybir as mybir
+
+K, T, S, M, L, H, N = 1024, 2048, 1024, 512, 512, 1024, 768
+FLOPS = 2 * (K * H * S + L * H * M + H * N * M)
+
+F32 = mybir.dt.float32
+BF16 = mybir.dt.bfloat16
+I32 = mybir.dt.int32
+U32 = mybir.dt.uint32
+U16 = mybir.dt.uint16
+U8 = mybir.dt.uint8
+E4M3 = mybir.dt.float8_e4m3fn_x4
+E2M1 = mybir.dt.float4_e2m1fn_x4
+ALU = mybir.AluOpType
+ACT = mybir.ActivationFunctionType
+
+P = 128
+PACK = 4
+PASS = P * PACK
+BANK = 512
+CHUNKS = ((512,), (256, 128, 128))
+
+
+def tile_list_ontology_facet_match_kernel(
+    tc, tab_words, tab_scales, offs, offs2, w1, wgt, tgt, wt_words, wt_scales, slope, gain, wo_words, wo_scales, out
+):
+    nc = tc.nc
+    with ExitStack() as ctx:
+        keep = ctx.enter_context(tc.tile_pool(name="keep", bufs=1))
+        work = ctx.enter_context(tc.tile_pool(name="work", bufs=2))
+        psum = ctx.enter_context(tc.psum_pool(name="psum", bufs=1))
+
+        def held(name, shape, dtype):
+            return keep.tile(shape, dtype, name=name, align_bytes=64)
+
+        def load_plane(name, scales, queue):
+            passes, width = scales.shape[0], scales.shape[2]
+            plane = held(name, [P, width // 4], I32)
+            nc.vector.memset(plane[:], 0)
+            for q in range(4):
+                queue.dma_start(
+                    out=plane[32 * q : 32 * q + 4 * passes, :], in_=scales[:, 4 * q : 4 * q + 4, :].bitcast(I32)
+                )
+            return plane[:].bitcast(U8)
+
+        def load_rows(name, src):
+            raw = held(name, [P, PACK, src.shape[1]], F32)
+            nc.sync.dma_start(out=raw[:], in_=src.rearrange("(p j) c -> p j c", j=PACK))
+            return raw
+
+        def load_words(name, src):
+            words = held(name, [P, src.shape[1] // 4], I32)
+            nc.sync.dma_start(out=words[:], in_=src.bitcast(I32))
+            return words
+
+        warm = held("warm", [P, 2], F32)
+        nc.vector.memset(warm[:, 0:1], 0.0)
+        nc.scalar.activation(out=warm[:, 1:2], in_=warm[:, 0:1], func=ACT.Exp)
+
+        tab_plane = load_plane("tab_plane", tab_scales, nc.scalar)
+        wt_plane = load_plane("wt_plane", wt_scales, nc.gpsimd)
+        wo_plane = load_plane("wo_plane", wo_scales, nc.gpsimd)
+
+        list1 = keep.tile([P, S // 16], U16, name="list1")
+        nc.sync.dma_start(list1[:], offs)
+        tab_raw = [None, None]
+        w1_raw = {}
+        half = PASS // 2
+        tab_raw[0] = load_words("tab0", tab_words[0].rearrange("p t i -> p (t i)"))
+        wt_raw = load_words("wt_raw", wt_words[0])
+        for u in range(2):
+            w1_raw[0, 0, u] = load_rows("w1_00%d" % u, w1[0:PASS, u * half : (u + 1) * half])
+        tab_raw[1] = load_words("tab1", tab_words[1].rearrange("p t i -> p (t i)"))
+        for u in range(2):
+            w1_raw[0, 1, u] = load_rows("w1_01%d" % u, w1[PASS : 2 * PASS, u * half : (u + 1) * half])
+        list2 = keep.tile([P, M // 16], U16, name="list2")
+        nc.sync.dma_start(list2[:], offs2)
+        wgt_sb = held("wgt_sb", [P, M], F32)
+        nc.sync.dma_start(out=wgt_sb[:], in_=wgt)
+        tgt_raw = [load_rows("tgt%d" % u, tgt[:, u * half : (u + 1) * half]) for u in range(2)]
+        slope_sb = held("slope_sb", [P, 2, PACK], F32)
+        nc.sync.dma_start(out=slope_sb[:], in_=slope.rearrange("(b p i) -> p b i", b=2, i=PACK))
+        gain_sb = held("gain_sb", [P, 2, PACK], F32)
+        nc.sync.dma_start(out=gain_sb[:], in_=gain.rearrange("(b p i) -> p b i", b=2, i=PACK))
+        for a in range(2):
+            for u in range(2):
+                w1_raw[1, a, u] = load_rows(
+                    "w1_1%d%d" % (a, u), w1[a * PASS : (a + 1) * PASS, PASS + u * half : PASS + (u + 1) * half]
+                )
+        wo_codes = [load_words("wo%d" % b, wo_words[b].rearrange("p c i -> p (c i)")) for b in range(2)]
+
+        def cast(engine, dst, src):
+            if engine == "scalar":
+                nc.scalar.copy(out=dst, in_=src)
+            else:
+                nc.vector.tensor_copy(out=dst, in_=src)
+
+        def quantise(name, grouped, width):
+            codes = held(name + "_codes", [P, width], U32)
+            plane = held(name + "_plane", [P, width], U8)
+            nc.vector.quantize_mx(out=codes[:].bitcast(E4M3), scales=plane[:], in_=grouped)
+            return codes, plane
+
+        v_codes = {}
+        v_plane = {}
+
+        def gather_words(a):
+            for s in range(2):
+                v_codes[a, s] = held("v%d%d" % (a, s), [P, BANK], U32)
+                nc.vector.tensor_copy(
+                    out=v_codes[a, s][:], in_=tab_raw[a][:].bitcast(U32).indirect(list1[:, 32 * s : 32 * (s + 1)])
+                )
+
+        w1_q = {}
+
+        def prepare_w1(b, a, engines):
+            grouped = work.tile([P, PACK, P, PACK], BF16, name="w1_grouped", align_bytes=64)
+            for u in range(2):
+                cast(
+                    engines[u],
+                    grouped[:, :, 64 * u : 64 * (u + 1), :].rearrange("p t m j -> p m j t"),
+                    w1_raw[b, a, u][:].rearrange("p j (m t) -> p m j t", t=PACK),
+                )
+            w1_q[b, a] = quantise("w1q%d%d" % (b, a), grouped[:].rearrange("p t m j -> p (t m j)"), PASS)
+
+        for s in range(2):
+            v_plane[s] = held("vs%d" % s, [P, BANK], U8)
+            nc.vector.tensor_copy(out=v_plane[s][:], in_=tab_plane.indirect(list1[:, 32 * s : 32 * (s + 1)]))
+        gather_words(0)
+        wt_codes = held("wt_codes", [P, H], U16)
+        nc.vector.tensor_copy(
+            out=wt_codes[:].rearrange("p (b i m) -> p b m i", b=2, i=PACK),
+            in_=wt_raw[:].bitcast(U16).rearrange("p (b m i) -> p b m i", b=2, i=PACK),
+        )
+        wt_scale = held("wt_scale", [P, H], U8)
+        nc.vector.tensor_copy(
+            out=wt_scale[:].rearrange("p (b i m) -> p b m i", b=2, i=PACK),
+            in_=wt_plane.rearrange("p (b m i) -> p b m i", b=2, i=PACK),
+        )
+
+        prepare_w1(0, 0, ("scalar", "scalar"))
+        gather_words(1)
+        prepare_w1(0, 1, ("scalar", "vector"))
+
+        h_sb = {}
+
+        def make_h(b, i):
+            h_sb[b, i] = held("h%d%d" % (b, i), [P, S], F32)
+            for s in range(2):
+                bank = psum.tile([P, BANK], F32, name="h_bank", bufs=4)
+                for a in range(2):
+                    codes, plane = w1_q[b, a]
+                    nc.tensor.matmul_mx(
+                        out=bank[:],
+                        lhsT=codes[:, P * i : P * (i + 1)].bitcast(E4M3),
+                        lhsT_scale=plane[:, P * i : P * (i + 1)],
+                        rhs=v_codes[a, s][:].bitcast(E4M3),
+                        rhs_scale=v_plane[s][4 * a :, :],
+                        start=(a == 0),
+                        stop=(a == 1),
+                    )
+                nc.scalar.copy(out=h_sb[b, i][:, BANK * s : BANK * (s + 1)], in_=bank[:])
+
+        make_h(0, 0)
+        make_h(0, 1)
+        tgt_grouped = held("tgt_grouped", [P, M, PACK], BF16)
+        for u in range(2):
+            cast(
+                ("scalar", "vector")[u],
+                tgt_grouped[:, half * u : half * (u + 1), :].rearrange("p (c i) j -> p c j i", i=4),
+                tgt_raw[u][:].rearrange("p j (c i) -> p c j i", i=4),
+            )
+        tgt_codes, tgt_plane = quantise("tgt", tgt_grouped[:].rearrange("p m j -> p (m j)"), M)
+        make_h(0, 2)
+        make_h(0, 3)
+
+        z_q = {}
+
+        def make_z(b, m0, width, between):
+            per_bank = BANK // width
+            e_sb = work.tile([P, PACK, width], F32, name="e_sb")
+            for i0 in range(0, PACK, per_bank):
+                x_sb = work.tile([P, per_bank, width], F32, name="x_sb", bufs=3)
+                bank = psum.tile([P, per_bank, width], F32, name="b_bank", bufs=2)
+                for n in range(per_bank):
+                    i = i0 + n
+                    nc.vector.tensor_tensor(
+                        out=x_sb[:, n, :],
+                        in0=h_sb[b, i][:].indirect(list2[:, m0 // 16 : (m0 + width) // 16]),
+                        in1=wgt_sb[:, m0 : m0 + width],
+                        op=ALU.mult,
+                    )
+                    cols = slice(PASS * b + P * i, PASS * b + P * (i + 1))
+                    nc.tensor.matmul_mx(
+                        out=bank[:, n, :],
+                        lhsT=wt_codes[:, cols].bitcast(E2M1),
+                        lhsT_scale=wt_scale[:, cols],
+                        rhs=tgt_codes[:, m0 : m0 + width].bitcast(E4M3),
+                        rhs_scale=tgt_plane[:, m0 : m0 + width],
+                        start=True,
+                        stop=True,
+                    )
+                d_sb = work.tile([P, per_bank, width], F32, name="d_sb", bufs=3)
+                nc.vector.tensor_tensor(out=d_sb[:], in0=bank[:], in1=x_sb[:], op=ALU.subtract)
+                sq_sb = work.tile([P, per_bank, width], F32, name="sq_sb", bufs=3)
+                nc.scalar.activation(out=sq_sb[:], in_=d_sb[:], func=ACT.Square)
+                for n in range(per_bank):
+                    i = i0 + n
+                    nc.scalar.activation(
+                        out=e_sb[:, i, :], in_=sq_sb[:, n, :], func=ACT.Exp, scale=slope_sb[:, b, i : i + 1]
+                    )
+                for job in between.get(i0, ()):
+                    job()
+            z_sb = work.tile([P, width, PACK], BF16, name="z_sb", align_bytes=64)
+            nc.vector.tensor_tensor(
+                out=z_sb[:].rearrange("p (c i) t -> p c t i", i=4),
+                in0=e_sb[:].rearrange("p t (c i) -> p c t i", i=4),
+                in1=gain_sb[:, b, :].unsqueeze(1).unsqueeze(3).to_broadcast([P, width // 4, PACK, 4]),
+                op=ALU.mult,
+            )
+            z_q[b, m0] = quantise("z%d_%d" % (b, m0), z_sb[:].rearrange("p m t -> p (m t)"), width)
+
+        def make_out(m0, width):
+            per_bank = BANK // width
+            tiles = N // P
+            staged = work.tile([P, tiles, width], F32, name="staged")
+            for turn, c0 in enumerate(range(0, tiles, per_bank)):
+                count = min(per_bank, tiles - c0)
+                bank = psum.tile([P, per_bank, width], F32, name="o_bank", bufs=2)
+                for n in range(count):
+                    cols = slice(P * (c0 + n), P * (c0 + n + 1))
+                    for b in range(2):
+                        codes, plane = z_q[b, 0] if b == 0 else z_q[b, m0]
+                        at = slice(m0, m0 + width) if b == 0 else slice(0, width)
+                        nc.tensor.matmul_mx(
+                            out=bank[:, n, :],
+                            lhsT=wo_codes[b][:, cols].bitcast(E4M3),
+                            lhsT_scale=wo_plane[4 * b :, cols],
+                            rhs=codes[:, at].bitcast(E4M3),
+                            rhs_scale=plane[:, at],
+                            start=(b == 0),
+                            stop=(b == 1),
+                        )
+                cast(("scalar", "vector")[turn % 2], staged[:, c0 : c0 + count, :], bank[:, 0:count, :])
+                nc.sync.dma_start(
+                    out=out.rearrange("(c p) m -> p c m", p=P)[:, c0 : c0 + count, m0 : m0 + width],
+                    in_=staged[:, c0 : c0 + count, :],
+                )
+
+        make_z(
+            0,
+            0,
+            M,
+            {
+                0: [lambda: prepare_w1(1, 0, ("scalar", "vector"))],
+                1: [lambda: prepare_w1(1, 1, ("scalar", "vector"))],
+                2: [lambda: make_h(1, 0), lambda: make_h(1, 1)],
+                3: [lambda: make_h(1, 2), lambda: make_h(1, 3)],
+            },
+        )
+        m0 = 0
+        for width in CHUNKS[1]:
+            make_z(1, m0, width, {})
+            make_out(m0, width)
+            m0 = m0 + width

@@ -20,7 +20,13 @@ P = 128
 PACK = 4
 PASS = P * PACK
 BANK = 512
-CHUNKS = ((512,), (256, 128, 128))
+CHUNKS = (256, 128, 128)
+W1_PIECES = {
+    (0, 0): ((512, "scalar"),),
+    (0, 1): ((384, "scalar"), (128, "vector")),
+    (1, 0): ((256, "scalar"), (256, "vector")),
+    (1, 1): ((256, "scalar"), (256, "vector")),
+}
 
 
 def tile_list_ontology_facet_match_kernel(
@@ -29,78 +35,99 @@ def tile_list_ontology_facet_match_kernel(
     nc = tc.nc
     with ExitStack() as ctx:
         keep = ctx.enter_context(tc.tile_pool(name="keep", bufs=1))
-        work = ctx.enter_context(tc.tile_pool(name="work", bufs=2))
         psum = ctx.enter_context(tc.psum_pool(name="psum", bufs=1))
 
         def held(name, shape, dtype):
             return keep.tile(shape, dtype, name=name, align_bytes=64)
 
-        def load_plane(name, scales, queue):
-            passes, width = scales.shape[0], scales.shape[2]
+        def bank_tile(number, shape):
+            return psum.tile(shape, F32, name="bank%d" % number)
+
+        def zeroed_plane(name, width):
             plane = held(name, [P, width // 4], I32)
-            nc.vector.memset(plane[:], 0)
+            nc.gpsimd.memset(plane[:], 0)
+            return plane
+
+        def load_plane(plane, scales, queue):
+            passes = scales.shape[0]
             for q in range(4):
                 queue.dma_start(
                     out=plane[32 * q : 32 * q + 4 * passes, :], in_=scales[:, 4 * q : 4 * q + 4, :].bitcast(I32)
                 )
-            return plane[:].bitcast(U8)
 
         def load_rows(name, src):
             raw = held(name, [P, PACK, src.shape[1]], F32)
             nc.sync.dma_start(out=raw[:], in_=src.rearrange("(p j) c -> p j c", j=PACK))
             return raw
 
-        def load_words(name, src):
-            words = held(name, [P, src.shape[1] // 4], I32)
-            nc.sync.dma_start(out=words[:], in_=src.bitcast(I32))
+        def load_words(name, src, pieces=1):
+            width = src.shape[1] // 4
+            words = held(name, [P, width], I32)
+            for first in range(0, width, width // pieces):
+                cols = slice(first, first + width // pieces)
+                nc.sync.dma_start(out=words[:, cols], in_=src.bitcast(I32)[:, cols])
             return words
 
-        warm = held("warm", [P, 2], F32)
-        nc.vector.memset(warm[:, 0:1], 0.0)
-        nc.scalar.activation(out=warm[:, 1:2], in_=warm[:, 0:1], func=ACT.Exp)
+        w1_raw = {}
 
-        tab_plane = load_plane("tab_plane", tab_scales, nc.scalar)
-        wt_plane = load_plane("wt_plane", wt_scales, nc.gpsimd)
-        wo_plane = load_plane("wo_plane", wo_scales, nc.gpsimd)
+        def load_w1(b, a):
+            w1_raw[b, a] = load_rows("w1_%d%d" % (b, a), w1[a * PASS : (a + 1) * PASS, b * PASS : (b + 1) * PASS])
 
+        tab_plane = zeroed_plane("tab_plane", T)
+        wt_plane = zeroed_plane("wt_plane", H)
+        wo_plane = zeroed_plane("wo_plane", N)
+
+        half = PASS // 2
+        tab_raw = [load_words("tab0", tab_words[0].rearrange("p t i -> p (t i)"), pieces=4)]
         list1 = keep.tile([P, S // 16], U16, name="list1")
         nc.sync.dma_start(list1[:], offs)
-        tab_raw = [None, None]
-        w1_raw = {}
-        half = PASS // 2
-        tab_raw[0] = load_words("tab0", tab_words[0].rearrange("p t i -> p (t i)"))
-        wt_raw = load_words("wt_raw", wt_words[0])
-        for u in range(2):
-            w1_raw[0, 0, u] = load_rows("w1_00%d" % u, w1[0:PASS, u * half : (u + 1) * half])
-        tab_raw[1] = load_words("tab1", tab_words[1].rearrange("p t i -> p (t i)"))
-        for u in range(2):
-            w1_raw[0, 1, u] = load_rows("w1_01%d" % u, w1[PASS : 2 * PASS, u * half : (u + 1) * half])
+        load_w1(0, 0)
         list2 = keep.tile([P, M // 16], U16, name="list2")
         nc.sync.dma_start(list2[:], offs2)
-        wgt_sb = held("wgt_sb", [P, M], F32)
-        nc.sync.dma_start(out=wgt_sb[:], in_=wgt)
-        tgt_raw = [load_rows("tgt%d" % u, tgt[:, u * half : (u + 1) * half]) for u in range(2)]
         slope_sb = held("slope_sb", [P, 2, PACK], F32)
         nc.sync.dma_start(out=slope_sb[:], in_=slope.rearrange("(b p i) -> p b i", b=2, i=PACK))
+        load_plane(tab_plane, tab_scales, nc.sync)
+        tab_raw.append(load_words("tab1", tab_words[1].rearrange("p t i -> p (t i)")))
+        load_w1(0, 1)
+        wt_raw = load_words("wt_raw", wt_words[0])
+        load_plane(wt_plane, wt_scales, nc.sync)
+        wgt_sb = held("wgt_sb", [P, M], F32)
+        nc.sync.dma_start(out=wgt_sb[:], in_=wgt)
+        tgt_raw = load_rows("tgt", tgt)
+        load_w1(1, 0)
+        load_w1(1, 1)
         gain_sb = held("gain_sb", [P, 2, PACK], F32)
         nc.sync.dma_start(out=gain_sb[:], in_=gain.rearrange("(b p i) -> p b i", b=2, i=PACK))
-        for a in range(2):
-            for u in range(2):
-                w1_raw[1, a, u] = load_rows(
-                    "w1_1%d%d" % (a, u), w1[a * PASS : (a + 1) * PASS, PASS + u * half : PASS + (u + 1) * half]
-                )
+        load_plane(wo_plane, wo_scales, nc.sync)
         wo_codes = [load_words("wo%d" % b, wo_words[b].rearrange("p c i -> p (c i)")) for b in range(2)]
 
-        def cast(engine, dst, src):
+        halves = held("halves", [P, 2, PACK], F32)
+        nc.gpsimd.memset(halves[:], 0.5)
+        minus_slope = held("minus_slope", [P, 2, PACK], F32)
+        nc.gpsimd.tensor_scalar(
+            out=minus_slope[:], in0=slope_sb[:], scalar1=-1.0, scalar2=0.0, op0=ALU.mult, op1=ALU.add
+        )
+        root = held("root", [P, 2, PACK], F32)
+        nc.gpsimd.tensor_tensor(out=root[:], in0=minus_slope[:], in1=halves[:], op=ALU.pow)
+
+        def copy_on(engine, dst, src):
             if engine == "scalar":
                 nc.scalar.copy(out=dst, in_=src)
             else:
                 nc.vector.tensor_copy(out=dst, in_=src)
 
-        def quantise(name, grouped, width):
-            codes = held(name + "_codes", [P, width], U32)
-            plane = held(name + "_plane", [P, width], U8)
-            nc.vector.quantize_mx(out=codes[:].bitcast(E4M3), scales=plane[:], in_=grouped)
+        def quantise(name, grouped, widths):
+            total = sum(widths)
+            codes = held(name + "_codes", [P, total], U32)
+            plane = held(name + "_plane", [P, total], U8)
+            first = 0
+            for width in widths:
+                nc.vector.quantize_mx(
+                    out=codes[:, first : first + width].bitcast(E4M3),
+                    scales=plane[:, first : first + width],
+                    in_=grouped[:, PACK * first : PACK * (first + width)],
+                )
+                first = first + width
             return codes, plane
 
         v_codes = {}
@@ -115,41 +142,37 @@ def tile_list_ontology_facet_match_kernel(
 
         w1_q = {}
 
-        def prepare_w1(b, a, engines):
-            grouped = work.tile([P, PACK, P, PACK], BF16, name="w1_grouped", align_bytes=64)
-            for u in range(2):
-                cast(
-                    engines[u],
-                    grouped[:, :, 64 * u : 64 * (u + 1), :].rearrange("p t m j -> p m j t"),
-                    w1_raw[b, a, u][:].rearrange("p j (m t) -> p m j t", t=PACK),
+        def prepare_w1(b, a, widths):
+            grouped = held("w1_grouped%d%d" % (b, a), [P, PACK * P * PACK], BF16)
+            view = grouped[:].rearrange("p (t m j) -> p m j t", t=PACK, j=PACK)
+            first = 0
+            for width, engine in W1_PIECES[b, a]:
+                copy_on(
+                    engine,
+                    view[:, first // PACK : (first + width) // PACK, :, :],
+                    w1_raw[b, a][:, :, first : first + width].rearrange("p j (m t) -> p m j t", t=PACK),
                 )
-            w1_q[b, a] = quantise("w1q%d%d" % (b, a), grouped[:].rearrange("p t m j -> p (t m j)"), PASS)
+                first = first + width
+            w1_q[b, a] = quantise("w1q%d%d" % (b, a), grouped, widths)
 
+        gather_words(0)
         for s in range(2):
             v_plane[s] = held("vs%d" % s, [P, BANK], U8)
-            nc.vector.tensor_copy(out=v_plane[s][:], in_=tab_plane.indirect(list1[:, 32 * s : 32 * (s + 1)]))
-        gather_words(0)
-        wt_codes = held("wt_codes", [P, H], U16)
-        nc.vector.tensor_copy(
-            out=wt_codes[:].rearrange("p (b i m) -> p b m i", b=2, i=PACK),
-            in_=wt_raw[:].bitcast(U16).rearrange("p (b m i) -> p b m i", b=2, i=PACK),
-        )
-        wt_scale = held("wt_scale", [P, H], U8)
-        nc.vector.tensor_copy(
-            out=wt_scale[:].rearrange("p (b i m) -> p b m i", b=2, i=PACK),
-            in_=wt_plane.rearrange("p (b m i) -> p b m i", b=2, i=PACK),
-        )
-
-        prepare_w1(0, 0, ("scalar", "scalar"))
+            nc.vector.tensor_copy(
+                out=v_plane[s][:], in_=tab_plane[:].bitcast(U8).indirect(list1[:, 32 * s : 32 * (s + 1)])
+            )
+        prepare_w1(0, 0, (PASS,))
+        warm = held("warm", [P, 1], F32)
+        nc.scalar.activation(out=warm[:], in_=w1_raw[0, 0][:, 0, 0:1], func=ACT.Exp, scale=0.0)
         gather_words(1)
-        prepare_w1(0, 1, ("scalar", "vector"))
+        prepare_w1(0, 1, (P, P, 2 * P))
 
         h_sb = {}
 
-        def make_h(b, i):
+        def make_h(b, i, first_bank):
             h_sb[b, i] = held("h%d%d" % (b, i), [P, S], F32)
             for s in range(2):
-                bank = psum.tile([P, BANK], F32, name="h_bank", bufs=4)
+                bank = bank_tile(first_bank + s, [P, BANK])
                 for a in range(2):
                     codes, plane = w1_q[b, a]
                     nc.tensor.matmul_mx(
@@ -161,40 +184,53 @@ def tile_list_ontology_facet_match_kernel(
                         start=(a == 0),
                         stop=(a == 1),
                     )
-                nc.scalar.copy(out=h_sb[b, i][:, BANK * s : BANK * (s + 1)], in_=bank[:])
+                copy_on("vector" if (b, i, s) == (0, 0, 1) else "scalar", h_sb[b, i][:, BANK * s : BANK * (s + 1)], bank[:])
 
-        make_h(0, 0)
-        make_h(0, 1)
-        tgt_grouped = held("tgt_grouped", [P, M, PACK], BF16)
+        make_h(0, 0, 0)
+        make_h(0, 1, 2)
+        wt_codes = keep.tile([P, H], U16, name="wt_codes", tag="w1_grouped01", align_bytes=64)
+        nc.vector.tensor_copy(
+            out=wt_codes[:].rearrange("p (b i m) -> p b i m", b=2, i=PACK),
+            in_=wt_raw[:].bitcast(U16).rearrange("p (b m i) -> p b i m", b=2, i=PACK),
+        )
+        wt_scale = keep.tile([P, H], U8, name="wt_scale", tag="w1_01", align_bytes=64)
+        nc.vector.tensor_copy(
+            out=wt_scale[:].rearrange("p (b i m) -> p b i m", b=2, i=PACK),
+            in_=wt_plane[:].bitcast(U8).rearrange("p (b m i) -> p b i m", b=2, i=PACK),
+        )
+        tgt_grouped = held("tgt_grouped", [P, M * PACK], BF16)
         for u in range(2):
-            cast(
-                ("scalar", "vector")[u],
-                tgt_grouped[:, half * u : half * (u + 1), :].rearrange("p (c i) j -> p c j i", i=4),
-                tgt_raw[u][:].rearrange("p j (c i) -> p c j i", i=4),
+            copy_on(
+                ("scalar", "scalar")[u],
+                tgt_grouped[:, PACK * half * u : PACK * half * (u + 1)].rearrange("p (c i j) -> p c j i", i=4, j=PACK),
+                tgt_raw[:, :, half * u : half * (u + 1)].rearrange("p j (c i) -> p c j i", i=4),
             )
-        tgt_codes, tgt_plane = quantise("tgt", tgt_grouped[:].rearrange("p m j -> p (m j)"), M)
-        make_h(0, 2)
-        make_h(0, 3)
+        tgt_codes, tgt_plane = quantise("tgt", tgt_grouped, (M,))
+        make_h(0, 2, 4)
+        prepare_w1(1, 0, (PASS,))
+        prepare_w1(1, 1, (PASS,))
+        make_h(0, 3, 0)
 
         z_q = {}
 
-        def make_z(b, m0, width, between):
+        d_tiles = {}
+
+        def make_d(b, m0, width, banks):
             per_bank = BANK // width
-            e_sb = work.tile([P, PACK, width], F32, name="e_sb")
-            for i0 in range(0, PACK, per_bank):
-                x_sb = work.tile([P, per_bank, width], F32, name="x_sb", bufs=3)
-                bank = psum.tile([P, per_bank, width], F32, name="b_bank", bufs=2)
+            for number, i0 in zip(banks, range(0, PACK, per_bank)):
+                x_sb = keep.tile([P, BANK], F32, name="x_sb", bufs=4)
+                bank = bank_tile(number, [P, BANK])
                 for n in range(per_bank):
                     i = i0 + n
                     nc.vector.tensor_tensor(
-                        out=x_sb[:, n, :],
+                        out=x_sb[:, n * width : (n + 1) * width],
                         in0=h_sb[b, i][:].indirect(list2[:, m0 // 16 : (m0 + width) // 16]),
                         in1=wgt_sb[:, m0 : m0 + width],
                         op=ALU.mult,
                     )
                     cols = slice(PASS * b + P * i, PASS * b + P * (i + 1))
                     nc.tensor.matmul_mx(
-                        out=bank[:, n, :],
+                        out=bank[:, n * width : (n + 1) * width],
                         lhsT=wt_codes[:, cols].bitcast(E2M1),
                         lhsT_scale=wt_scale[:, cols],
                         rhs=tgt_codes[:, m0 : m0 + width].bitcast(E4M3),
@@ -202,66 +238,72 @@ def tile_list_ontology_facet_match_kernel(
                         start=True,
                         stop=True,
                     )
-                d_sb = work.tile([P, per_bank, width], F32, name="d_sb", bufs=3)
+                d_sb = held("d%d_%d_%d" % (b, m0, i0), [P, BANK], F32)
                 nc.vector.tensor_tensor(out=d_sb[:], in0=bank[:], in1=x_sb[:], op=ALU.subtract)
-                sq_sb = work.tile([P, per_bank, width], F32, name="sq_sb", bufs=3)
-                nc.scalar.activation(out=sq_sb[:], in_=d_sb[:], func=ACT.Square)
                 for n in range(per_bank):
-                    i = i0 + n
-                    nc.scalar.activation(
-                        out=e_sb[:, i, :], in_=sq_sb[:, n, :], func=ACT.Exp, scale=slope_sb[:, b, i : i + 1]
-                    )
-                for job in between.get(i0, ()):
-                    job()
-            z_sb = work.tile([P, width, PACK], BF16, name="z_sb", align_bytes=64)
-            nc.vector.tensor_tensor(
-                out=z_sb[:].rearrange("p (c i) t -> p c t i", i=4),
-                in0=e_sb[:].rearrange("p t (c i) -> p c t i", i=4),
-                in1=gain_sb[:, b, :].unsqueeze(1).unsqueeze(3).to_broadcast([P, width // 4, PACK, 4]),
-                op=ALU.mult,
-            )
-            z_q[b, m0] = quantise("z%d_%d" % (b, m0), z_sb[:].rearrange("p m t -> p (m t)"), width)
+                    d_tiles[b, m0, i0 + n] = d_sb[:, n * width : (n + 1) * width]
 
-        def make_out(m0, width):
-            per_bank = BANK // width
-            tiles = N // P
-            staged = work.tile([P, tiles, width], F32, name="staged")
-            for turn, c0 in enumerate(range(0, tiles, per_bank)):
-                count = min(per_bank, tiles - c0)
-                bank = psum.tile([P, per_bank, width], F32, name="o_bank", bufs=2)
-                for n in range(count):
-                    cols = slice(P * (c0 + n), P * (c0 + n + 1))
-                    for b in range(2):
-                        codes, plane = z_q[b, 0] if b == 0 else z_q[b, m0]
-                        at = slice(m0, m0 + width) if b == 0 else slice(0, width)
+        def make_z(b, m0, width):
+            name = "%d_%d" % (b, m0)
+            sq_sb = held("sq" + name, [P, PACK, width], F32)
+            for i in range(PACK):
+                nc.scalar.activation(
+                    out=sq_sb[:, i, :], in_=d_tiles[b, m0, i], func=ACT.Square, scale=root[:, b, i : i + 1]
+                )
+            e_sb = held("e" + name, [P, width, PACK], F32)
+            z_sb = held("z" + name, [P, width * PACK], BF16)
+            step = min(width, half)
+            for first in range(0, width, step):
+                cols = slice(first, first + step)
+                nc.scalar.activation(
+                    out=e_sb[:, cols, :].rearrange("p (c i) t -> p c t i", i=4),
+                    in_=sq_sb[:, :, cols].rearrange("p t (c i) -> p c t i", i=4),
+                    func=ACT.Exp,
+                    scale=-1.0,
+                )
+                nc.vector.tensor_tensor(
+                    out=z_sb[:, PACK * first : PACK * (first + step)].rearrange("p (m t) -> p m t", t=PACK),
+                    in0=e_sb[:, cols, :],
+                    in1=gain_sb[:, b, :].unsqueeze(1).to_broadcast([P, step, PACK]),
+                    op=ALU.mult,
+                )
+            z_q[b, m0] = quantise("z" + name, z_sb, (width,))
+
+        def make_out(m0, width, banks):
+            count = N // P // len(banks)
+            for turn, number in enumerate(banks):
+                c0 = turn * count
+                bank = bank_tile(number, [P, count, width])
+                for b in range(2):
+                    codes, plane = z_q[b, 0] if b == 0 else z_q[b, m0]
+                    at = slice(m0, m0 + width) if b == 0 else slice(0, width)
+                    for n in range(count):
+                        cols = slice(P * (c0 + n), P * (c0 + n + 1))
                         nc.tensor.matmul_mx(
                             out=bank[:, n, :],
                             lhsT=wo_codes[b][:, cols].bitcast(E4M3),
-                            lhsT_scale=wo_plane[4 * b :, cols],
+                            lhsT_scale=wo_plane[:].bitcast(U8)[4 * b :, cols],
                             rhs=codes[:, at].bitcast(E4M3),
                             rhs_scale=plane[:, at],
-                            start=(b == 0),
-                            stop=(b == 1),
+                            start=(b == 0 and n == 0),
+                            stop=(b == 1 and n == count - 1),
                         )
-                cast(("scalar", "vector")[turn % 2], staged[:, c0 : c0 + count, :], bank[:, 0:count, :])
+                staged = held("staged%d_%d" % (m0, c0), [P, count, width], F32)
+                last = m0 + width == M and turn == 1
+                copy_on("vector" if last else "scalar", staged[:], bank[:])
                 nc.sync.dma_start(
-                    out=out.rearrange("(c p) m -> p c m", p=P)[:, c0 : c0 + count, m0 : m0 + width],
-                    in_=staged[:, c0 : c0 + count, :],
+                    out=out.rearrange("(c p) m -> p c m", p=P)[:, c0 : c0 + count, m0 : m0 + width], in_=staged[:]
                 )
 
-        make_z(
-            0,
-            0,
-            M,
-            {
-                0: [lambda: prepare_w1(1, 0, ("scalar", "vector"))],
-                1: [lambda: prepare_w1(1, 1, ("scalar", "vector"))],
-                2: [lambda: make_h(1, 0), lambda: make_h(1, 1)],
-                3: [lambda: make_h(1, 2), lambda: make_h(1, 3)],
-            },
-        )
+        make_d(0, 0, M, (6, 7, 2, 3))
+        make_h(1, 0, 4)
+        make_h(1, 1, 0)
+        make_h(1, 2, 6)
+        make_h(1, 3, 2)
+        make_z(0, 0, M)
         m0 = 0
-        for width in CHUNKS[1]:
-            make_z(1, m0, width, {})
-            make_out(m0, width)
+        for width, z_banks, out_banks in zip(CHUNKS, ((4, 5), (0,), (1,)), ((6, 7, 2), (3, 4), (5, 0))):
+            make_d(1, m0, width, z_banks)
+            make_z(1, m0, width)
+            make_out(m0, width, out_banks)
             m0 = m0 + width

@@ -21,9 +21,11 @@ PACK = 4
 PASS = P * PACK
 BANK = 512
 CHUNKS = (256, 128, 128)
+X_TAGS = {}
+Z_TAGS = {(0, 256): "e1_0", (0, 384): "e1_256"}
 W1_PIECES = {
     (0, 0): ((512, "scalar"),),
-    (0, 1): ((384, "scalar"), (128, "vector")),
+    (0, 1): ((320, "scalar"), (192, "vector")),
     (1, 0): ((256, "scalar"), (256, "vector")),
     (1, 1): ((256, "scalar"), (256, "vector")),
 }
@@ -78,14 +80,14 @@ def tile_list_ontology_facet_match_kernel(
         wo_plane = zeroed_plane("wo_plane", N)
 
         half = PASS // 2
+        slope_sb = held("slope_sb", [P, 2, PACK], F32)
+        nc.sync.dma_start(out=slope_sb[:], in_=slope.rearrange("(b p i) -> p b i", b=2, i=PACK))
         tab_raw = [load_words("tab0", tab_words[0].rearrange("p t i -> p (t i)"), pieces=4)]
         list1 = keep.tile([P, S // 16], U16, name="list1")
         nc.sync.dma_start(list1[:], offs)
         load_w1(0, 0)
         list2 = keep.tile([P, M // 16], U16, name="list2")
         nc.sync.dma_start(list2[:], offs2)
-        slope_sb = held("slope_sb", [P, 2, PACK], F32)
-        nc.sync.dma_start(out=slope_sb[:], in_=slope.rearrange("(b p i) -> p b i", b=2, i=PACK))
         load_plane(tab_plane, tab_scales, nc.sync)
         tab_raw.append(load_words("tab1", tab_words[1].rearrange("p t i -> p (t i)")))
         load_w1(0, 1)
@@ -100,15 +102,6 @@ def tile_list_ontology_facet_match_kernel(
         nc.sync.dma_start(out=gain_sb[:], in_=gain.rearrange("(b p i) -> p b i", b=2, i=PACK))
         load_plane(wo_plane, wo_scales, nc.sync)
         wo_codes = [load_words("wo%d" % b, wo_words[b].rearrange("p c i -> p (c i)")) for b in range(2)]
-
-        halves = held("halves", [P, 2, PACK], F32)
-        nc.gpsimd.memset(halves[:], 0.5)
-        minus_slope = held("minus_slope", [P, 2, PACK], F32)
-        nc.gpsimd.tensor_scalar(
-            out=minus_slope[:], in0=slope_sb[:], scalar1=-1.0, scalar2=0.0, op0=ALU.mult, op1=ALU.add
-        )
-        root = held("root", [P, 2, PACK], F32)
-        nc.gpsimd.tensor_tensor(out=root[:], in0=minus_slope[:], in1=halves[:], op=ALU.pow)
 
         def copy_on(engine, dst, src):
             if engine == "scalar":
@@ -162,8 +155,6 @@ def tile_list_ontology_facet_match_kernel(
                 out=v_plane[s][:], in_=tab_plane[:].bitcast(U8).indirect(list1[:, 32 * s : 32 * (s + 1)])
             )
         prepare_w1(0, 0, (PASS,))
-        warm = held("warm", [P, 1], F32)
-        nc.scalar.activation(out=warm[:], in_=w1_raw[0, 0][:, 0, 0:1], func=ACT.Exp, scale=0.0)
         gather_words(1)
         prepare_w1(0, 1, (P, P, 2 * P))
 
@@ -184,7 +175,7 @@ def tile_list_ontology_facet_match_kernel(
                         start=(a == 0),
                         stop=(a == 1),
                     )
-                copy_on("vector" if (b, i, s) == (0, 0, 1) else "scalar", h_sb[b, i][:, BANK * s : BANK * (s + 1)], bank[:])
+                copy_on("scalar", h_sb[b, i][:, BANK * s : BANK * (s + 1)], bank[:])
 
         make_h(0, 0, 0)
         make_h(0, 1, 2)
@@ -207,9 +198,9 @@ def tile_list_ontology_facet_match_kernel(
             )
         tgt_codes, tgt_plane = quantise("tgt", tgt_grouped, (M,))
         make_h(0, 2, 4)
+        make_h(0, 3, 0)
         prepare_w1(1, 0, (PASS,))
         prepare_w1(1, 1, (PASS,))
-        make_h(0, 3, 0)
 
         z_q = {}
 
@@ -218,7 +209,8 @@ def tile_list_ontology_facet_match_kernel(
         def make_d(b, m0, width, banks):
             per_bank = BANK // width
             for number, i0 in zip(banks, range(0, PACK, per_bank)):
-                x_sb = keep.tile([P, BANK], F32, name="x_sb", bufs=4)
+                x_name = "x%d_%d_%d" % (b, m0, i0)
+                x_sb = keep.tile([P, BANK], F32, name=x_name, tag=X_TAGS.get((b, m0), x_name), align_bytes=64)
                 bank = bank_tile(number, [P, BANK])
                 for n in range(per_bank):
                     i = i0 + n
@@ -240,33 +232,35 @@ def tile_list_ontology_facet_match_kernel(
                     )
                 d_sb = held("d%d_%d_%d" % (b, m0, i0), [P, BANK], F32)
                 nc.vector.tensor_tensor(out=d_sb[:], in0=bank[:], in1=x_sb[:], op=ALU.subtract)
+                d_tiles[b, m0, i0] = d_sb
+
+        e_tiles = {}
+
+        def gaussian(b, m0, width):
+            per_bank = BANK // width
+            e_sb = held("e%d_%d" % (b, m0), [P, PACK, width], F32)
+            e_tiles[b] = (m0, e_sb)
+            for i0 in range(0, PACK, per_bank):
+                sq_sb = held("sq%d_%d_%d" % (b, m0, i0), [P, BANK], F32)
+                nc.scalar.activation(out=sq_sb[:], in_=d_tiles[b, m0, i0][:], func=ACT.Square)
                 for n in range(per_bank):
-                    d_tiles[b, m0, i0 + n] = d_sb[:, n * width : (n + 1) * width]
+                    nc.scalar.activation(
+                        out=e_sb[:, i0 + n, :],
+                        in_=sq_sb[:, n * width : (n + 1) * width],
+                        func=ACT.Exp,
+                        scale=slope_sb[:, b, i0 + n : i0 + n + 1],
+                    )
 
         def make_z(b, m0, width):
             name = "%d_%d" % (b, m0)
-            sq_sb = held("sq" + name, [P, PACK, width], F32)
-            for i in range(PACK):
-                nc.scalar.activation(
-                    out=sq_sb[:, i, :], in_=d_tiles[b, m0, i], func=ACT.Square, scale=root[:, b, i : i + 1]
-                )
-            e_sb = held("e" + name, [P, width, PACK], F32)
-            z_sb = held("z" + name, [P, width * PACK], BF16)
-            step = min(width, half)
-            for first in range(0, width, step):
-                cols = slice(first, first + step)
-                nc.scalar.activation(
-                    out=e_sb[:, cols, :].rearrange("p (c i) t -> p c t i", i=4),
-                    in_=sq_sb[:, :, cols].rearrange("p t (c i) -> p c t i", i=4),
-                    func=ACT.Exp,
-                    scale=-1.0,
-                )
-                nc.vector.tensor_tensor(
-                    out=z_sb[:, PACK * first : PACK * (first + step)].rearrange("p (m t) -> p m t", t=PACK),
-                    in0=e_sb[:, cols, :],
-                    in1=gain_sb[:, b, :].unsqueeze(1).to_broadcast([P, step, PACK]),
-                    op=ALU.mult,
-                )
+            first, e_sb = e_tiles[b]
+            z_sb = keep.tile([P, width * PACK], BF16, name="z" + name, tag=Z_TAGS.get((b, m0), "z" + name), align_bytes=64)
+            nc.vector.tensor_tensor(
+                out=z_sb[:].rearrange("p (c i t) -> p c t i", i=4, t=PACK),
+                in0=e_sb[:, :, m0 - first : m0 - first + width].rearrange("p t (c i) -> p c t i", i=4),
+                in1=gain_sb[:, b, :].unsqueeze(1).unsqueeze(3).to_broadcast([P, width // 4, PACK, 4]),
+                op=ALU.mult,
+            )
             z_q[b, m0] = quantise("z" + name, z_sb, (width,))
 
         def make_out(m0, width, banks):
@@ -275,16 +269,15 @@ def tile_list_ontology_facet_match_kernel(
                 c0 = turn * count
                 bank = bank_tile(number, [P, count, width])
                 for b in range(2):
-                    codes, plane = z_q[b, 0] if b == 0 else z_q[b, m0]
-                    at = slice(m0, m0 + width) if b == 0 else slice(0, width)
+                    codes, plane = z_q[b, m0]
                     for n in range(count):
                         cols = slice(P * (c0 + n), P * (c0 + n + 1))
                         nc.tensor.matmul_mx(
                             out=bank[:, n, :],
                             lhsT=wo_codes[b][:, cols].bitcast(E4M3),
                             lhsT_scale=wo_plane[:].bitcast(U8)[4 * b :, cols],
-                            rhs=codes[:, at].bitcast(E4M3),
-                            rhs_scale=plane[:, at],
+                            rhs=codes[:].bitcast(E4M3),
+                            rhs_scale=plane[:],
                             start=(b == 0 and n == 0),
                             stop=(b == 1 and n == count - 1),
                         )
@@ -296,14 +289,16 @@ def tile_list_ontology_facet_match_kernel(
                 )
 
         make_d(0, 0, M, (6, 7, 2, 3))
+        gaussian(0, 0, M)
         make_h(1, 0, 4)
         make_h(1, 1, 0)
         make_h(1, 2, 6)
         make_h(1, 3, 2)
-        make_z(0, 0, M)
         m0 = 0
         for width, z_banks, out_banks in zip(CHUNKS, ((4, 5), (0,), (1,)), ((6, 7, 2), (3, 4), (5, 0))):
             make_d(1, m0, width, z_banks)
+            make_z(0, m0, width)
+            gaussian(1, m0, width)
             make_z(1, m0, width)
             make_out(m0, width, out_banks)
             m0 = m0 + width

@@ -20,14 +20,13 @@ P = 128
 PACK = 4
 PASS = P * PACK
 BANK = 512
-CHUNKS = (256, 128, 128)
-X_TAGS = {}
-Z_TAGS = {(0, 256): "e1_0", (0, 384): "e1_256"}
+X_TAGS = {(1, 2): "x00", (1, 3): "x02"}
+H_TAGS = {(0, 2): "w1_100"}
 W1_PIECES = {
-    (0, 0): ((512, "scalar"),),
-    (0, 1): ((320, "scalar"), (192, "vector")),
-    (1, 0): ((256, "scalar"), (256, "vector")),
-    (1, 1): ((256, "scalar"), (256, "vector")),
+    (0, 0): ((256, "scalar"), (256, "scalar")),
+    (0, 1): ((256, "scalar"), (256, "vector")),
+    (1, 0): ((512, "scalar"),),
+    (1, 1): ((512, "vector"),),
 }
 
 
@@ -39,15 +38,15 @@ def tile_list_ontology_facet_match_kernel(
         keep = ctx.enter_context(tc.tile_pool(name="keep", bufs=1))
         psum = ctx.enter_context(tc.psum_pool(name="psum", bufs=1))
 
-        def held(name, shape, dtype):
-            return keep.tile(shape, dtype, name=name, align_bytes=64)
+        def held(name, shape, dtype, tag=None):
+            return keep.tile(shape, dtype, name=name, tag=tag or name, align_bytes=64)
 
         def bank_tile(number, shape):
             return psum.tile(shape, F32, name="bank%d" % number)
 
         def zeroed_plane(name, width):
             plane = held(name, [P, width // 4], I32)
-            nc.gpsimd.memset(plane[:], 0)
+            nc.vector.memset(plane[:], 0)
             return plane
 
         def load_plane(plane, scales, queue):
@@ -70,36 +69,42 @@ def tile_list_ontology_facet_match_kernel(
                 nc.sync.dma_start(out=words[:, cols], in_=src.bitcast(I32)[:, cols])
             return words
 
+        def load_by_row(name, vec):
+            tile = held(name, [P, 2, PACK], F32)
+            nc.sync.dma_start(out=tile[:], in_=vec.rearrange("(b p i) -> p b i", b=2, i=PACK))
+            return tile
+
         w1_raw = {}
 
-        def load_w1(b, a):
-            w1_raw[b, a] = load_rows("w1_%d%d" % (b, a), w1[a * PASS : (a + 1) * PASS, b * PASS : (b + 1) * PASS])
+        def load_w1(b, a, pieces=1):
+            width = PASS // pieces
+            for u in range(pieces):
+                first = b * PASS + u * width
+                raw = load_rows("w1_%d%d%d" % (b, a, u), w1[a * PASS : (a + 1) * PASS, first : first + width])
+                w1_raw[b, a, u] = raw
+            w1_raw[b, a] = width
 
         tab_plane = zeroed_plane("tab_plane", T)
         wt_plane = zeroed_plane("wt_plane", H)
-        wo_plane = zeroed_plane("wo_plane", N)
-
-        half = PASS // 2
-        slope_sb = held("slope_sb", [P, 2, PACK], F32)
-        nc.sync.dma_start(out=slope_sb[:], in_=slope.rearrange("(b p i) -> p b i", b=2, i=PACK))
-        tab_raw = [load_words("tab0", tab_words[0].rearrange("p t i -> p (t i)"), pieces=4)]
         list1 = keep.tile([P, S // 16], U16, name="list1")
         nc.sync.dma_start(list1[:], offs)
-        load_w1(0, 0)
+        slope_sb = load_by_row("slope_sb", slope)
+        gain_sb = load_by_row("gain_sb", gain)
         list2 = keep.tile([P, M // 16], U16, name="list2")
         nc.sync.dma_start(list2[:], offs2)
+        tab_raw = [load_words("tab0", tab_words[0].rearrange("p t i -> p (t i)"), pieces=4)]
         load_plane(tab_plane, tab_scales, nc.sync)
+        load_w1(0, 0, 2)
         tab_raw.append(load_words("tab1", tab_words[1].rearrange("p t i -> p (t i)")))
-        load_w1(0, 1)
+        load_w1(0, 1, 2)
         wt_raw = load_words("wt_raw", wt_words[0])
         load_plane(wt_plane, wt_scales, nc.sync)
         wgt_sb = held("wgt_sb", [P, M], F32)
         nc.sync.dma_start(out=wgt_sb[:], in_=wgt)
-        tgt_raw = load_rows("tgt", tgt)
         load_w1(1, 0)
         load_w1(1, 1)
-        gain_sb = held("gain_sb", [P, 2, PACK], F32)
-        nc.sync.dma_start(out=gain_sb[:], in_=gain.rearrange("(b p i) -> p b i", b=2, i=PACK))
+        tgt_raw = load_rows("tgt", tgt)
+        wo_plane = held("wo_plane", [P, N // 4], I32)
         load_plane(wo_plane, wo_scales, nc.sync)
         wo_codes = [load_words("wo%d" % b, wo_words[b].rearrange("p c i -> p (c i)")) for b in range(2)]
 
@@ -109,9 +114,9 @@ def tile_list_ontology_facet_match_kernel(
             else:
                 nc.vector.tensor_copy(out=dst, in_=src)
 
-        def quantise(name, grouped, widths):
+        def quantise(name, grouped, widths, tag=None):
             total = sum(widths)
-            codes = held(name + "_codes", [P, total], U32)
+            codes = held(name + "_codes", [P, total], U32, tag=tag)
             plane = held(name + "_plane", [P, total], U8)
             first = 0
             for width in widths:
@@ -124,144 +129,116 @@ def tile_list_ontology_facet_match_kernel(
             return codes, plane
 
         v_codes = {}
-        v_plane = {}
 
-        def gather_words(a):
-            for s in range(2):
-                v_codes[a, s] = held("v%d%d" % (a, s), [P, BANK], U32)
+        def gather_words(a, pieces):
+            v_codes[a] = held("v%d" % a, [P, S], U32, tag=("v0", "w1_001")[a])
+            width = S // pieces
+            for first in range(0, S, width):
                 nc.vector.tensor_copy(
-                    out=v_codes[a, s][:], in_=tab_raw[a][:].bitcast(U32).indirect(list1[:, 32 * s : 32 * (s + 1)])
+                    out=v_codes[a][:, first : first + width],
+                    in_=tab_raw[a][:].bitcast(U32).indirect(list1[:, first // 16 : (first + width) // 16]),
                 )
 
+        w1_grouped = {}
         w1_q = {}
 
-        def prepare_w1(b, a, widths):
-            grouped = held("w1_grouped%d%d" % (b, a), [P, PACK * P * PACK], BF16)
-            view = grouped[:].rearrange("p (t m j) -> p m j t", t=PACK, j=PACK)
+        def round_w1(b, a, only=None):
+            if (b, a) not in w1_grouped:
+                w1_grouped[b, a] = held("w1_grouped%d%d" % (b, a), [P, PACK * P * PACK], BF16)
+            view = w1_grouped[b, a][:].rearrange("p (t m j) -> p m j t", t=PACK, j=PACK)
             first = 0
+            loaded = w1_raw[b, a]
             for width, engine in W1_PIECES[b, a]:
-                copy_on(
-                    engine,
-                    view[:, first // PACK : (first + width) // PACK, :, :],
-                    w1_raw[b, a][:, :, first : first + width].rearrange("p j (m t) -> p m j t", t=PACK),
-                )
+                if only in (None, engine):
+                    local = first % loaded
+                    copy_on(
+                        engine,
+                        view[:, first // PACK : (first + width) // PACK, :, :],
+                        w1_raw[b, a, first // loaded][:, :, local : local + width].rearrange(
+                            "p j (m t) -> p m j t", t=PACK
+                        ),
+                    )
                 first = first + width
-            w1_q[b, a] = quantise("w1q%d%d" % (b, a), grouped, widths)
 
-        gather_words(0)
-        for s in range(2):
-            v_plane[s] = held("vs%d" % s, [P, BANK], U8)
-            nc.vector.tensor_copy(
-                out=v_plane[s][:], in_=tab_plane[:].bitcast(U8).indirect(list1[:, 32 * s : 32 * (s + 1)])
-            )
-        prepare_w1(0, 0, (PASS,))
-        gather_words(1)
-        prepare_w1(0, 1, (P, P, 2 * P))
+        def quantise_w1(b, a, widths, tag=None):
+            w1_q[b, a] = quantise("w1q%d%d" % (b, a), w1_grouped[b, a], widths, tag)
+
+        gather_words(0, 1)
+        v_plane = held("v_plane", [P, S], U8)
+        nc.vector.tensor_copy(out=v_plane[:], in_=tab_plane[:].bitcast(U8).indirect(list1[:]))
+        round_w1(0, 0)
+        quantise_w1(0, 0, (PASS,))
+        gather_words(1, 1)
+        round_w1(0, 1)
+        quantise_w1(0, 1, (P, P, 2 * P))
 
         h_sb = {}
 
         def make_h(b, i, first_bank):
-            h_sb[b, i] = held("h%d%d" % (b, i), [P, S], F32)
+            h_sb[b, i] = held("h%d%d" % (b, i), [P, S], F32, tag=H_TAGS.get((b, i)))
             for s in range(2):
                 bank = bank_tile(first_bank + s, [P, BANK])
+                cols = slice(BANK * s, BANK * (s + 1))
                 for a in range(2):
                     codes, plane = w1_q[b, a]
                     nc.tensor.matmul_mx(
                         out=bank[:],
                         lhsT=codes[:, P * i : P * (i + 1)].bitcast(E4M3),
                         lhsT_scale=plane[:, P * i : P * (i + 1)],
-                        rhs=v_codes[a, s][:].bitcast(E4M3),
-                        rhs_scale=v_plane[s][4 * a :, :],
+                        rhs=v_codes[a][:, cols].bitcast(E4M3),
+                        rhs_scale=v_plane[4 * a :, cols],
                         start=(a == 0),
                         stop=(a == 1),
                     )
-                copy_on("scalar", h_sb[b, i][:, BANK * s : BANK * (s + 1)], bank[:])
+                nc.scalar.copy(out=h_sb[b, i][:, cols], in_=bank[:])
 
-        make_h(0, 0, 0)
-        make_h(0, 1, 2)
-        wt_codes = keep.tile([P, H], U16, name="wt_codes", tag="w1_grouped01", align_bytes=64)
-        nc.vector.tensor_copy(
-            out=wt_codes[:].rearrange("p (b i m) -> p b i m", b=2, i=PACK),
-            in_=wt_raw[:].bitcast(U16).rearrange("p (b m i) -> p b i m", b=2, i=PACK),
-        )
-        wt_scale = keep.tile([P, H], U8, name="wt_scale", tag="w1_01", align_bytes=64)
-        nc.vector.tensor_copy(
-            out=wt_scale[:].rearrange("p (b i m) -> p b i m", b=2, i=PACK),
-            in_=wt_plane[:].bitcast(U8).rearrange("p (b m i) -> p b i m", b=2, i=PACK),
-        )
-        tgt_grouped = held("tgt_grouped", [P, M * PACK], BF16)
-        for u in range(2):
-            copy_on(
-                ("scalar", "scalar")[u],
-                tgt_grouped[:, PACK * half * u : PACK * half * (u + 1)].rearrange("p (c i j) -> p c j i", i=4, j=PACK),
-                tgt_raw[:, :, half * u : half * (u + 1)].rearrange("p j (c i) -> p c j i", i=4),
+        x_sb = {}
+
+        def pick(b, i):
+            x_sb[b, i] = held("x%d%d" % (b, i), [P, M], F32, tag=X_TAGS.get((b, i)))
+            nc.vector.tensor_tensor(out=x_sb[b, i][:], in0=h_sb[b, i][:].indirect(list2[:]), in1=wgt_sb[:], op=ALU.mult)
+
+        d_sb = [held("d%d" % b, [P, PACK, M], F32) for b in range(2)]
+
+        def subtract(b, i, number):
+            bank = bank_tile(number, [P, BANK])
+            cols = slice(PASS * b + P * i, PASS * b + P * (i + 1))
+            nc.tensor.matmul_mx(
+                out=bank[:],
+                lhsT=wt_codes[:, cols].bitcast(E2M1),
+                lhsT_scale=wt_scale[:, cols],
+                rhs=tgt_codes[:].bitcast(E4M3),
+                rhs_scale=tgt_plane[:],
+                start=True,
+                stop=True,
             )
-        tgt_codes, tgt_plane = quantise("tgt", tgt_grouped, (M,))
-        make_h(0, 2, 4)
-        make_h(0, 3, 0)
-        prepare_w1(1, 0, (PASS,))
-        prepare_w1(1, 1, (PASS,))
+            nc.vector.tensor_tensor(out=d_sb[b][:, i, :], in0=bank[:], in1=x_sb[b, i][:], op=ALU.subtract)
+
+        sq_sb = [held("sq%d" % b, [P, PACK, M], F32, tag=("v0", "tab1")[b]) for b in range(2)]
+        e_first = held("e0", [P, PACK, M], F32, tag="w1_110")
+        e_second = [held("e1%d" % u, [P, PACK, M // 2], F32) for u in range(2)]
+
+        def gaussian(b, planes, cols, target):
+            nc.scalar.activation(out=sq_sb[b][:, planes, cols], in_=d_sb[b][:, planes, cols], func=ACT.Square)
+            for i in range(planes.start, planes.stop):
+                nc.scalar.activation(
+                    out=target[:, i, :], in_=sq_sb[b][:, i, cols], func=ACT.Exp, scale=slope_sb[:, b, i : i + 1]
+                )
 
         z_q = {}
 
-        d_tiles = {}
-
-        def make_d(b, m0, width, banks):
-            per_bank = BANK // width
-            for number, i0 in zip(banks, range(0, PACK, per_bank)):
-                x_name = "x%d_%d_%d" % (b, m0, i0)
-                x_sb = keep.tile([P, BANK], F32, name=x_name, tag=X_TAGS.get((b, m0), x_name), align_bytes=64)
-                bank = bank_tile(number, [P, BANK])
-                for n in range(per_bank):
-                    i = i0 + n
-                    nc.vector.tensor_tensor(
-                        out=x_sb[:, n * width : (n + 1) * width],
-                        in0=h_sb[b, i][:].indirect(list2[:, m0 // 16 : (m0 + width) // 16]),
-                        in1=wgt_sb[:, m0 : m0 + width],
-                        op=ALU.mult,
-                    )
-                    cols = slice(PASS * b + P * i, PASS * b + P * (i + 1))
-                    nc.tensor.matmul_mx(
-                        out=bank[:, n * width : (n + 1) * width],
-                        lhsT=wt_codes[:, cols].bitcast(E2M1),
-                        lhsT_scale=wt_scale[:, cols],
-                        rhs=tgt_codes[:, m0 : m0 + width].bitcast(E4M3),
-                        rhs_scale=tgt_plane[:, m0 : m0 + width],
-                        start=True,
-                        stop=True,
-                    )
-                d_sb = held("d%d_%d_%d" % (b, m0, i0), [P, BANK], F32)
-                nc.vector.tensor_tensor(out=d_sb[:], in0=bank[:], in1=x_sb[:], op=ALU.subtract)
-                d_tiles[b, m0, i0] = d_sb
-
-        e_tiles = {}
-
-        def gaussian(b, m0, width):
-            per_bank = BANK // width
-            e_sb = held("e%d_%d" % (b, m0), [P, PACK, width], F32)
-            e_tiles[b] = (m0, e_sb)
-            for i0 in range(0, PACK, per_bank):
-                sq_sb = held("sq%d_%d_%d" % (b, m0, i0), [P, BANK], F32)
-                nc.scalar.activation(out=sq_sb[:], in_=d_tiles[b, m0, i0][:], func=ACT.Square)
-                for n in range(per_bank):
-                    nc.scalar.activation(
-                        out=e_sb[:, i0 + n, :],
-                        in_=sq_sb[:, n * width : (n + 1) * width],
-                        func=ACT.Exp,
-                        scale=slope_sb[:, b, i0 + n : i0 + n + 1],
-                    )
-
-        def make_z(b, m0, width):
-            name = "%d_%d" % (b, m0)
-            first, e_sb = e_tiles[b]
-            z_sb = keep.tile([P, width * PACK], BF16, name="z" + name, tag=Z_TAGS.get((b, m0), "z" + name), align_bytes=64)
+        def make_z(b, m0, width, source, tag=None):
+            name = "z%d_%d" % (b, m0)
+            z_sb = held(name, [P, width * PACK], BF16, tag=tag)
             nc.vector.tensor_tensor(
                 out=z_sb[:].rearrange("p (c i t) -> p c t i", i=4, t=PACK),
-                in0=e_sb[:, :, m0 - first : m0 - first + width].rearrange("p t (c i) -> p c t i", i=4),
+                in0=source.rearrange("p t (c i) -> p c t i", i=4),
                 in1=gain_sb[:, b, :].unsqueeze(1).unsqueeze(3).to_broadcast([P, width // 4, PACK, 4]),
                 op=ALU.mult,
             )
-            z_q[b, m0] = quantise("z" + name, z_sb, (width,))
+            codes, plane = quantise(name, z_sb, (width,))
+            for first in range(0, width, P):
+                z_q[b, m0 + first] = (codes, plane, first)
 
         def make_out(m0, width, banks):
             count = N // P // len(banks)
@@ -269,36 +246,84 @@ def tile_list_ontology_facet_match_kernel(
                 c0 = turn * count
                 bank = bank_tile(number, [P, count, width])
                 for b in range(2):
-                    codes, plane = z_q[b, m0]
+                    codes, plane, first = z_q[b, m0]
                     for n in range(count):
                         cols = slice(P * (c0 + n), P * (c0 + n + 1))
                         nc.tensor.matmul_mx(
                             out=bank[:, n, :],
                             lhsT=wo_codes[b][:, cols].bitcast(E4M3),
                             lhsT_scale=wo_plane[:].bitcast(U8)[4 * b :, cols],
-                            rhs=codes[:].bitcast(E4M3),
-                            rhs_scale=plane[:],
+                            rhs=codes[:, first : first + width].bitcast(E4M3),
+                            rhs_scale=plane[:, first : first + width],
                             start=(b == 0 and n == 0),
                             stop=(b == 1 and n == count - 1),
                         )
                 staged = held("staged%d_%d" % (m0, c0), [P, count, width], F32)
-                last = m0 + width == M and turn == 1
+                last = m0 > 0 and turn == 1
                 copy_on("vector" if last else "scalar", staged[:], bank[:])
                 nc.sync.dma_start(
                     out=out.rearrange("(c p) m -> p c m", p=P)[:, c0 : c0 + count, m0 : m0 + width], in_=staged[:]
                 )
 
-        make_d(0, 0, M, (6, 7, 2, 3))
-        gaussian(0, 0, M)
-        make_h(1, 0, 4)
-        make_h(1, 1, 0)
-        make_h(1, 2, 6)
-        make_h(1, 3, 2)
-        m0 = 0
-        for width, z_banks, out_banks in zip(CHUNKS, ((4, 5), (0,), (1,)), ((6, 7, 2), (3, 4), (5, 0))):
-            make_d(1, m0, width, z_banks)
-            make_z(0, m0, width)
-            gaussian(1, m0, width)
-            make_z(1, m0, width)
-            make_out(m0, width, out_banks)
-            m0 = m0 + width
+        make_h(0, 0, 0)
+        wt_codes = held("wt_codes", [P, H], U16, tag="w1_grouped01")
+        nc.vector.tensor_copy(
+            out=wt_codes[:].rearrange("p (b i m) -> p b i m", b=2, i=PACK),
+            in_=wt_raw[:].bitcast(U16).rearrange("p (b m i) -> p b i m", b=2, i=PACK),
+        )
+        wt_scale = held("wt_scale", [P, H], U8, tag="w1_011")
+        nc.vector.tensor_copy(
+            out=wt_scale[:].rearrange("p (b i m) -> p b i m", b=2, i=PACK),
+            in_=wt_plane[:].bitcast(U8).rearrange("p (b m i) -> p b i m", b=2, i=PACK),
+        )
+        tgt_grouped = held("tgt_grouped", [P, M * PACK], BF16)
+        half = M // 2
+
+        def round_tgt(u, engine):
+            copy_on(
+                engine,
+                tgt_grouped[:, PACK * half * u : PACK * half * (u + 1)].rearrange("p (c i j) -> p c j i", i=4, j=PACK),
+                tgt_raw[:, :, half * u : half * (u + 1)].rearrange("p j (c i) -> p c j i", i=4),
+            )
+
+        pick(0, 0)
+        make_h(0, 1, 2)
+        pick(0, 1)
+        round_w1(1, 0)
+        round_w1(1, 1)
+        quantise_w1(1, 0, (PASS,))
+        quantise_w1(1, 1, (PASS,))
+        make_h(0, 2, 4)
+        pick(0, 2)
+        make_h(0, 3, 6)
+        pick(0, 3)
+        make_h(1, 0, 0)
+        round_tgt(0, "scalar")
+        round_tgt(1, "vector")
+        pick(1, 0)
+        tgt_codes, tgt_plane = quantise("tgt", tgt_grouped, (M,))
+        make_h(1, 1, 2)
+        pick(1, 1)
+        make_h(1, 2, 4)
+        make_h(1, 3, 6)
+        subtract(0, 0, 0)
+        subtract(0, 1, 1)
+        pick(1, 2)
+        subtract(0, 2, 2)
+        subtract(0, 3, 3)
+        pick(1, 3)
+        for i in range(PACK):
+            subtract(1, i, 4 + i)
+        for i in range(PACK):
+            gaussian(0, slice(i, i + 1), slice(0, M), e_first)
+        for i in range(PACK):
+            gaussian(1, slice(i, i + 1), slice(0, half), e_second[0])
+        make_z(0, 0, half, e_first[:, :, 0:half])
+        make_z(1, 0, half, e_second[0][:])
+        for i in range(0, PACK, 2):
+            gaussian(1, slice(i, i + 2), slice(half, M), e_second[1])
+        make_out(0, half, (0, 1, 2))
+        make_z(0, half, half, e_first[:, :, half:M], tag="e10")
+        for m0, banks in ((half, (3, 4)), (half + P, (5, 6))):
+            make_z(1, m0, P, e_second[1][:, :, m0 - half : m0 - half + P])
+            make_out(m0, P, banks)

@@ -20,11 +20,13 @@ P = 128
 PACK = 4
 PASS = P * PACK
 BANK = 512
-X_TAGS = {(1, 2): "x00", (1, 3): "x02"}
+X_TAGS = {(0, 2): "h01", (1, 2): "x00", (1, 3): "x03"}
 H_TAGS = {(0, 2): "w1_100"}
+G_TAGS = {(1, 1): "h01"}
+PLACES = {"w1_110": 0, "w1q10_codes": 0, "tgt_grouped0": 2048, "e0": 0}
 W1_PIECES = {
     (0, 0): ((256, "scalar"), (256, "scalar")),
-    (0, 1): ((256, "scalar"), (256, "vector")),
+    (0, 1): ((256, "scalar"), (96, "scalar"), (160, "vector")),
     (1, 0): ((512, "scalar"),),
     (1, 1): ((512, "vector"),),
 }
@@ -38,7 +40,11 @@ def tile_list_ontology_facet_match_kernel(
         keep = ctx.enter_context(tc.tile_pool(name="keep", bufs=1))
         psum = ctx.enter_context(tc.psum_pool(name="psum", bufs=1))
 
+        shared = ctx.enter_context(tc.tile_pool(name="shared", bufs=1))
+
         def held(name, shape, dtype, tag=None):
+            if name in PLACES:
+                return shared.tile(shape, dtype, name=name, align_bytes=64, offset=PLACES[name])
             return keep.tile(shape, dtype, name=name, tag=tag or name, align_bytes=64)
 
         def bank_tile(number, shape):
@@ -144,7 +150,7 @@ def tile_list_ontology_facet_match_kernel(
 
         def round_w1(b, a, only=None):
             if (b, a) not in w1_grouped:
-                w1_grouped[b, a] = held("w1_grouped%d%d" % (b, a), [P, PACK * P * PACK], BF16)
+                w1_grouped[b, a] = held("w1_grouped%d%d" % (b, a), [P, PACK * P * PACK], BF16, tag=G_TAGS.get((b, a)))
             view = w1_grouped[b, a][:].rearrange("p (t m j) -> p m j t", t=PACK, j=PACK)
             first = 0
             loaded = w1_raw[b, a]
@@ -179,7 +185,7 @@ def tile_list_ontology_facet_match_kernel(
             for s in range(2):
                 bank = bank_tile(first_bank + s, [P, BANK])
                 cols = slice(BANK * s, BANK * (s + 1))
-                for a in range(2):
+                for a in (b, 1 - b):
                     codes, plane = w1_q[b, a]
                     nc.tensor.matmul_mx(
                         out=bank[:],
@@ -187,8 +193,8 @@ def tile_list_ontology_facet_match_kernel(
                         lhsT_scale=plane[:, P * i : P * (i + 1)],
                         rhs=v_codes[a][:, cols].bitcast(E4M3),
                         rhs_scale=v_plane[4 * a :, cols],
-                        start=(a == 0),
-                        stop=(a == 1),
+                        start=(a == b),
+                        stop=(a != b),
                     )
                 nc.scalar.copy(out=h_sb[b, i][:, cols], in_=bank[:])
 
@@ -276,32 +282,40 @@ def tile_list_ontology_facet_match_kernel(
             out=wt_scale[:].rearrange("p (b i m) -> p b i m", b=2, i=PACK),
             in_=wt_plane[:].bitcast(U8).rearrange("p (b m i) -> p b i m", b=2, i=PACK),
         )
-        tgt_grouped = held("tgt_grouped", [P, M * PACK], BF16)
         half = M // 2
+        tgt_grouped = {}
+        tgt_codes = held("tgt_codes", [P, M], U32)
+        tgt_plane = held("tgt_plane", [P, M], U8)
 
-        def round_tgt(u, engine):
+        def quantise_tgt(u):
+            cols = slice(half * u, half * (u + 1))
+            nc.vector.quantize_mx(out=tgt_codes[:, cols].bitcast(E4M3), scales=tgt_plane[:, cols], in_=tgt_grouped[u][:])
+
+        def round_tgt(u, engine, tag):
+            tgt_grouped[u] = held("tgt_grouped%d" % u, [P, half * PACK], BF16, tag=tag)
             copy_on(
                 engine,
-                tgt_grouped[:, PACK * half * u : PACK * half * (u + 1)].rearrange("p (c i j) -> p c j i", i=4, j=PACK),
+                tgt_grouped[u][:].rearrange("p (c i j) -> p c j i", i=4, j=PACK),
                 tgt_raw[:, :, half * u : half * (u + 1)].rearrange("p j (c i) -> p c j i", i=4),
             )
 
         pick(0, 0)
         make_h(0, 1, 2)
         pick(0, 1)
-        round_w1(1, 0)
-        round_w1(1, 1)
-        quantise_w1(1, 0, (PASS,))
-        quantise_w1(1, 1, (PASS,))
-        make_h(0, 2, 4)
-        pick(0, 2)
         make_h(0, 3, 6)
         pick(0, 3)
+        round_w1(1, 0)
+        round_w1(1, 1)
+        quantise_w1(1, 1, (PASS,))
+        quantise_w1(1, 0, (PASS,), "w1_110")
+        make_h(0, 2, 4)
+        pick(0, 2)
         make_h(1, 0, 0)
-        round_tgt(0, "scalar")
-        round_tgt(1, "vector")
+        round_tgt(0, "scalar", "w1_grouped10")
+        quantise_tgt(0)
+        round_tgt(1, "vector", "w1_100")
         pick(1, 0)
-        tgt_codes, tgt_plane = quantise("tgt", tgt_grouped, (M,))
+        quantise_tgt(1)
         make_h(1, 1, 2)
         pick(1, 1)
         make_h(1, 2, 4)
@@ -309,12 +323,12 @@ def tile_list_ontology_facet_match_kernel(
         subtract(0, 0, 0)
         subtract(0, 1, 1)
         pick(1, 2)
-        subtract(0, 2, 2)
-        subtract(0, 3, 3)
+        subtract(0, 3, 2)
+        subtract(0, 2, 3)
         pick(1, 3)
         for i in range(PACK):
             subtract(1, i, 4 + i)
-        for i in range(PACK):
+        for i in (0, 1, 3, 2):
             gaussian(0, slice(i, i + 1), slice(0, M), e_first)
         for i in range(PACK):
             gaussian(1, slice(i, i + 1), slice(0, half), e_second[0])

@@ -20,10 +20,11 @@ P = 128
 PACK = 4
 PASS = P * PACK
 BANK = 512
-X_TAGS = {(0, 2): "h01", (1, 2): "x00", (1, 3): "x03"}
-H_TAGS = {(0, 2): "w1_100"}
+X_TAGS = {(0, 3): "w1_grouped10"}
+H_TAGS = {(0, 3): "w1_100"}
 G_TAGS = {(1, 1): "h01"}
 PLACES = {"w1_110": 0, "w1q10_codes": 0, "tgt_grouped0": 2048, "e0": 0}
+OUT_BANKS = ((0, 1), (2, 3), (6, 7), (4, 5))
 W1_PIECES = {
     (0, 0): ((256, "scalar"), (256, "scalar")),
     (0, 1): ((256, "scalar"), (96, "scalar"), (160, "vector")),
@@ -92,13 +93,22 @@ def tile_list_ontology_facet_match_kernel(
 
         tab_plane = zeroed_plane("tab_plane", T)
         wt_plane = zeroed_plane("wt_plane", H)
+        tab_raw = [held("tab0", [P, T], I32)]
+        first_pass = tab_words[0].rearrange("p t i -> p (t i)").bitcast(I32)
+
+        def load_first_pass(pieces):
+            for piece in pieces:
+                cols = slice(piece * T // 4, (piece + 1) * T // 4)
+                nc.sync.dma_start(out=tab_raw[0][:, cols], in_=first_pass[:, cols])
+
+        load_first_pass((0, 1))
         list1 = keep.tile([P, S // 16], U16, name="list1")
         nc.sync.dma_start(list1[:], offs)
         slope_sb = load_by_row("slope_sb", slope)
         gain_sb = load_by_row("gain_sb", gain)
         list2 = keep.tile([P, M // 16], U16, name="list2")
         nc.sync.dma_start(list2[:], offs2)
-        tab_raw = [load_words("tab0", tab_words[0].rearrange("p t i -> p (t i)"), pieces=4)]
+        load_first_pass((2, 3))
         load_plane(tab_plane, tab_scales, nc.sync)
         load_w1(0, 0, 2)
         tab_raw.append(load_words("tab1", tab_words[1].rearrange("p t i -> p (t i)")))
@@ -120,19 +130,24 @@ def tile_list_ontology_facet_match_kernel(
             else:
                 nc.vector.tensor_copy(out=dst, in_=src)
 
-        def quantise(name, grouped, widths, tag=None):
-            total = sum(widths)
-            codes = held(name + "_codes", [P, total], U32, tag=tag)
-            plane = held(name + "_plane", [P, total], U8)
+        def start_quantise(name, total):
+            return held(name + "_codes", [P, total], U32), held(name + "_plane", [P, total], U8)
+
+        def quantise_part(target, grouped, first, width):
+            codes, plane = target
+            nc.vector.quantize_mx(
+                out=codes[:, first : first + width].bitcast(E4M3),
+                scales=plane[:, first : first + width],
+                in_=grouped[:, PACK * first : PACK * (first + width)],
+            )
+
+        def quantise(name, grouped, widths):
+            target = start_quantise(name, sum(widths))
             first = 0
             for width in widths:
-                nc.vector.quantize_mx(
-                    out=codes[:, first : first + width].bitcast(E4M3),
-                    scales=plane[:, first : first + width],
-                    in_=grouped[:, PACK * first : PACK * (first + width)],
-                )
+                quantise_part(target, grouped, first, width)
                 first = first + width
-            return codes, plane
+            return target
 
         v_codes = {}
 
@@ -166,8 +181,8 @@ def tile_list_ontology_facet_match_kernel(
                     )
                 first = first + width
 
-        def quantise_w1(b, a, widths, tag=None):
-            w1_q[b, a] = quantise("w1q%d%d" % (b, a), w1_grouped[b, a], widths, tag)
+        def quantise_w1(b, a, widths):
+            w1_q[b, a] = quantise("w1q%d%d" % (b, a), w1_grouped[b, a], widths)
 
         gather_words(0, 1)
         v_plane = held("v_plane", [P, S], U8)
@@ -198,47 +213,66 @@ def tile_list_ontology_facet_match_kernel(
                     )
                 nc.scalar.copy(out=h_sb[b, i][:, cols], in_=bank[:])
 
-        x_sb = {}
+        x_first = {}
+        x_pair = {}
 
         def pick(b, i):
-            x_sb[b, i] = held("x%d%d" % (b, i), [P, M], F32, tag=X_TAGS.get((b, i)))
-            nc.vector.tensor_tensor(out=x_sb[b, i][:], in0=h_sb[b, i][:].indirect(list2[:]), in1=wgt_sb[:], op=ALU.mult)
+            if b == 0:
+                x_first[i] = held("x0%d" % i, [P, M], F32, tag=X_TAGS.get((b, i)))
+                target = x_first[i][:]
+            else:
+                if i % 2 == 0:
+                    x_pair[i // 2] = held("x1_%d" % (i // 2), [P, 2, M], F32, tag=(None, "x00")[i // 2])
+                target = x_pair[i // 2][:, i % 2, :]
+            nc.vector.tensor_tensor(out=target, in0=h_sb[b, i][:].indirect(list2[:]), in1=wgt_sb[:], op=ALU.mult)
 
         d_sb = [held("d%d" % b, [P, PACK, M], F32) for b in range(2)]
 
-        def subtract(b, i, number):
-            bank = bank_tile(number, [P, BANK])
-            cols = slice(PASS * b + P * i, PASS * b + P * (i + 1))
+        def target_product(bank, b, i, cols):
+            rows = slice(PASS * b + P * i, PASS * b + P * (i + 1))
             nc.tensor.matmul_mx(
-                out=bank[:],
-                lhsT=wt_codes[:, cols].bitcast(E2M1),
-                lhsT_scale=wt_scale[:, cols],
-                rhs=tgt_codes[:].bitcast(E4M3),
-                rhs_scale=tgt_plane[:],
+                out=bank,
+                lhsT=wt_codes[:, rows].bitcast(E2M1),
+                lhsT_scale=wt_scale[:, rows],
+                rhs=tgt_codes[:, cols].bitcast(E4M3),
+                rhs_scale=tgt_plane[:, cols],
                 start=True,
                 stop=True,
             )
-            nc.vector.tensor_tensor(out=d_sb[b][:, i, :], in0=bank[:], in1=x_sb[b, i][:], op=ALU.subtract)
 
-        sq_sb = [held("sq%d" % b, [P, PACK, M], F32, tag=("v0", "tab1")[b]) for b in range(2)]
-        e_first = held("e0", [P, PACK, M], F32, tag="w1_110")
-        e_second = [held("e1%d" % u, [P, PACK, M // 2], F32) for u in range(2)]
+        def subtract(i, number):
+            bank = bank_tile(number, [P, BANK])
+            target_product(bank[:], 0, i, slice(0, M))
+            nc.vector.tensor_tensor(out=d_sb[0][:, i, :], in0=bank[:], in1=x_first[i][:], op=ALU.subtract)
 
-        def gaussian(b, planes, cols, target):
-            nc.scalar.activation(out=sq_sb[b][:, planes, cols], in_=d_sb[b][:, planes, cols], func=ACT.Square)
-            for i in range(planes.start, planes.stop):
+        def subtract_pair(pair, u, number):
+            cols = slice(half * u, half * (u + 1))
+            bank = bank_tile(number, [P, 2, half])
+            for n in range(2):
+                target_product(bank[:, n, :], 1, 2 * pair + n, cols)
+            nc.vector.tensor_tensor(
+                out=d_sb[1][:, 2 * pair : 2 * pair + 2, cols], in0=bank[:], in1=x_pair[pair][:, :, cols], op=ALU.subtract
+            )
+
+        sq_first = held("sq0", [P, PACK, M], F32, tag="v0")
+        e_sb = [held("e%d" % b, [P, PACK, M], F32) for b in range(2)]
+
+        def gaussian(b, first, count, cols, squares):
+            nc.scalar.activation(out=squares, in_=d_sb[b][:, first : first + count, cols], func=ACT.Square)
+            for n in range(count):
+                i = first + n
                 nc.scalar.activation(
-                    out=target[:, i, :], in_=sq_sb[b][:, i, cols], func=ACT.Exp, scale=slope_sb[:, b, i : i + 1]
+                    out=e_sb[b][:, i, cols], in_=squares[:, n, :], func=ACT.Exp, scale=slope_sb[:, b, i : i + 1]
                 )
 
         z_q = {}
 
-        def make_z(b, m0, width, source, tag=None):
+        def make_z(b, m0, width, tag=None):
             name = "z%d_%d" % (b, m0)
             z_sb = held(name, [P, width * PACK], BF16, tag=tag)
             nc.vector.tensor_tensor(
                 out=z_sb[:].rearrange("p (c i t) -> p c t i", i=4, t=PACK),
-                in0=source.rearrange("p t (c i) -> p c t i", i=4),
+                in0=e_sb[b][:, :, m0 : m0 + width].rearrange("p t (c i) -> p c t i", i=4),
                 in1=gain_sb[:, b, :].unsqueeze(1).unsqueeze(3).to_broadcast([P, width // 4, PACK, 4]),
                 op=ALU.mult,
             )
@@ -265,7 +299,7 @@ def tile_list_ontology_facet_match_kernel(
                             stop=(b == 1 and n == count - 1),
                         )
                 staged = held("staged%d_%d" % (m0, c0), [P, count, width], F32)
-                last = m0 > 0 and turn == 1
+                last = m0 + width == M and turn == 1
                 copy_on("vector" if last else "scalar", staged[:], bank[:])
                 nc.sync.dma_start(
                     out=out.rearrange("(c p) m -> p c m", p=P)[:, c0 : c0 + count, m0 : m0 + width], in_=staged[:]
@@ -302,42 +336,50 @@ def tile_list_ontology_facet_match_kernel(
         pick(0, 0)
         make_h(0, 1, 2)
         pick(0, 1)
-        make_h(0, 3, 6)
-        pick(0, 3)
-        round_w1(1, 0)
-        round_w1(1, 1)
-        quantise_w1(1, 1, (PASS,))
-        quantise_w1(1, 0, (PASS,), "w1_110")
         make_h(0, 2, 4)
         pick(0, 2)
-        make_h(1, 0, 0)
-        round_tgt(0, "scalar", "w1_grouped10")
+        round_w1(1, 0)
+        round_w1(1, 1)
+        prepared = [start_quantise("w1q1%d" % a, PASS) for a in range(2)]
+        for first, width in ((0, P), (P, P), (2 * P, 2 * P)):
+            for a in (1, 0):
+                quantise_part(prepared[a], w1_grouped[1, a], first, width)
+        for a in range(2):
+            w1_q[1, a] = prepared[a]
+        make_h(0, 3, 4)
+        round_tgt(0, "scalar", None)
+        round_tgt(1, "vector", "h01")
         quantise_tgt(0)
-        round_tgt(1, "vector", "w1_100")
-        pick(1, 0)
         quantise_tgt(1)
+        pick(0, 3)
+        make_h(1, 0, 0)
+        pick(1, 0)
         make_h(1, 1, 2)
         pick(1, 1)
-        make_h(1, 2, 4)
-        make_h(1, 3, 6)
-        subtract(0, 0, 0)
-        subtract(0, 1, 1)
+        make_h(1, 2, 6)
+        make_h(1, 3, 4)
+        subtract(0, 0)
+        subtract(1, 1)
         pick(1, 2)
-        subtract(0, 3, 2)
-        subtract(0, 2, 3)
+        subtract(2, 2)
+        subtract(3, 3)
+        subtract_pair(0, 0, 6)
         pick(1, 3)
+        subtract_pair(0, 1, 7)
+        subtract_pair(1, 0, 4)
         for i in range(PACK):
-            subtract(1, i, 4 + i)
-        for i in (0, 1, 3, 2):
-            gaussian(0, slice(i, i + 1), slice(0, M), e_first)
-        for i in range(PACK):
-            gaussian(1, slice(i, i + 1), slice(0, half), e_second[0])
-        make_z(0, 0, half, e_first[:, :, 0:half])
-        make_z(1, 0, half, e_second[0][:])
-        for i in range(0, PACK, 2):
-            gaussian(1, slice(i, i + 2), slice(half, M), e_second[1])
-        make_out(0, half, (0, 1, 2))
-        make_z(0, half, half, e_first[:, :, half:M], tag="e10")
-        for m0, banks in ((half, (3, 4)), (half + P, (5, 6))):
-            make_z(1, m0, P, e_second[1][:, :, m0 - half : m0 - half + P])
-            make_out(m0, P, banks)
+            gaussian(0, i, 1, slice(0, M), sq_first[:, i : i + 1, :])
+        make_z(0, 0, P)
+        subtract_pair(1, 1, 5)
+        for u in range(2):
+            squares = held("sq1_pair%d" % u, [P, 2, half], F32)
+            gaussian(1, 0, 2, slice(half * u, half * (u + 1)), squares[:])
+            for m0 in range(half * u, half * (u + 1), P):
+                squares = held("sq1_%d" % m0, [P, 2, P], F32)
+                gaussian(1, 2, 2, slice(m0, m0 + P), squares[:])
+        make_z(0, P, P)
+        for m0 in range(0, M, P):
+            if m0 > P:
+                make_z(0, m0, P, tag="sq1_%d" % (m0 - P))
+            make_z(1, m0, P)
+            make_out(m0, P, OUT_BANKS[m0 // P])

@@ -270,15 +270,24 @@ def tile_list_ontology_facet_match_kernel(
         def make_z(b, m0, width, tag=None):
             name = "z%d_%d" % (b, m0)
             z_sb = held(name, [P, width * PACK], BF16, tag=tag)
+            if b == 0:
+                nc.vector.tensor_copy(
+                    out=z_sb[:].rearrange("p (c i t) -> p c t i", i=4, t=PACK),
+                    in_=z_planes[:, :, m0 : m0 + width].rearrange("p t (c i) -> p c t i", i=4),
+                )
+            else:
+                weigh(b, m0, width, z_sb)
+            codes, plane = quantise(name, z_sb, (width,))
+            for first in range(0, width, P):
+                z_q[b, m0 + first] = (codes, plane, first)
+
+        def weigh(b, m0, width, z_sb):
             nc.vector.tensor_tensor(
                 out=z_sb[:].rearrange("p (c i t) -> p c t i", i=4, t=PACK),
                 in0=e_sb[b][:, :, m0 : m0 + width].rearrange("p t (c i) -> p c t i", i=4),
                 in1=gain_sb[:, b, :].unsqueeze(1).unsqueeze(3).to_broadcast([P, width // 4, PACK, 4]),
                 op=ALU.mult,
             )
-            codes, plane = quantise(name, z_sb, (width,))
-            for first in range(0, width, P):
-                z_q[b, m0 + first] = (codes, plane, first)
 
         def make_out(m0, width, banks):
             count = N // P // len(banks)
@@ -367,10 +376,19 @@ def tile_list_ontology_facet_match_kernel(
         pick(1, 3)
         subtract_pair(0, 1, 7)
         subtract_pair(1, 0, 4)
+        z_planes = held("z_planes", [P, PACK, M], BF16, tag="h12")
         for i in range(PACK):
             gaussian(0, i, 1, slice(0, M), sq_first[:, i : i + 1, :])
-        make_z(0, 0, P)
+            nc.gpsimd.tensor_scalar(
+                out=z_planes[:, i, :],
+                in0=e_sb[0][:, i, :],
+                scalar1=gain_sb[:, 0, i : i + 1],
+                scalar2=0.0,
+                op0=ALU.mult,
+                op1=ALU.add,
+            )
         subtract_pair(1, 1, 5)
+        make_z(0, 0, P)
         for u in range(2):
             squares = held("sq1_pair%d" % u, [P, 2, half], F32)
             gaussian(1, 0, 2, slice(half * u, half * (u + 1)), squares[:])

@@ -21,12 +21,20 @@ PACK = 4
 PASS = P * PACK
 BANK = 512
 X_TAGS = {(0, 3): "w1_grouped10"}
-H_TAGS = {(0, 3): "w1_100"}
 G_TAGS = {(1, 1): "h01"}
-PLACES = {"w1_110": 0, "w1q10_codes": 0, "tgt_grouped0": 2048, "e0": 0}
+PLACES = {
+    "w1_110": 0, "w1q10_codes": 0, "tgt_grouped0": 2048, "e0": 0,
+    "tab1": 8128, "tgt1": 8192, "tgt0": 12288, "h10": 12288,
+    "w1_000": 24448, "w1_100": 32576, "h03": 32832,
+    "tab0": 40768, "wgt_sb": 40768, "wt_raw": 42816,
+    "w1_grouped01": 57344, "wt_codes": 57344,
+    "w1_grouped00": 61440, "v1": 61440,
+    "tab_rows": 65536, "w1_010": 67520,
+    "wo0": 67584, "wo1": 70656, "wo_plane": 73728, "slope_sb": 74496, "gain_sb": 74560, "wt_scale": 74624,
+}
 OUT_BANKS = ((0, 1), (2, 3), (6, 7), (4, 5))
 W1_PIECES = {
-    (0, 0): ((256, "scalar"), (256, "scalar")),
+    (0, 0): ((320, "scalar"), (192, "vector")),
     (0, 1): ((256, "scalar"), (96, "scalar"), (160, "vector")),
     (1, 0): ((512, "scalar"),),
     (1, 1): ((512, "vector"),),
@@ -50,11 +58,6 @@ def tile_list_ontology_facet_match_kernel(
 
         def bank_tile(number, shape):
             return psum.tile(shape, F32, name="bank%d" % number)
-
-        def zeroed_plane(name, width):
-            plane = held(name, [P, width // 4], I32)
-            nc.vector.memset(plane[:], 0)
-            return plane
 
         def load_plane(plane, scales, queue):
             passes = scales.shape[0]
@@ -85,41 +88,58 @@ def tile_list_ontology_facet_match_kernel(
 
         def load_w1(b, a, pieces=1):
             width = PASS // pieces
-            for u in range(pieces):
-                first = b * PASS + u * width
-                raw = load_rows("w1_%d%d%d" % (b, a, u), w1[a * PASS : (a + 1) * PASS, first : first + width])
-                w1_raw[b, a, u] = raw
-            w1_raw[b, a] = width
+            raw = held("w1_%d%d0" % (b, a), [P, PACK, PASS], F32)
+            block = w1[a * PASS : (a + 1) * PASS, b * PASS : (b + 1) * PASS].rearrange("(p j) c -> p j c", j=PACK)
+            for first in range(0, PASS, width):
+                nc.sync.dma_start(out=raw[:, :, first : first + width], in_=block[:, :, first : first + width])
+            w1_raw[b, a, 0] = raw
+            w1_raw[b, a] = PASS
 
-        tab_plane = zeroed_plane("tab_plane", T)
-        wt_plane = zeroed_plane("wt_plane", H)
-        tab_raw = [held("tab0", [P, T], I32)]
-        first_pass = tab_words[0].rearrange("p t i -> p (t i)").bitcast(I32)
-
-        def load_first_pass(pieces):
-            for piece in pieces:
-                cols = slice(piece * T // 4, (piece + 1) * T // 4)
-                nc.sync.dma_start(out=tab_raw[0][:, cols], in_=first_pass[:, cols])
-
-        load_first_pass((0, 1))
+        tab_rows = held("tab_rows", [P, T // 4], I32)
+        for a in range(2):
+            nc.sync.dma_start(
+                out=tab_rows[16 * a : 16 * (a + 1), :],
+                in_=tab_scales[a].bitcast(I32).rearrange("(q r) t -> r q t", r=4),
+            )
+        nc.vector.memset(tab_rows[32:64, :], 0)
+        nc.vector.memset(tab_rows[64:, :], 0)
         list1 = keep.tile([P, S // 16], U16, name="list1")
         nc.sync.dma_start(list1[:], offs)
-        slope_sb = load_by_row("slope_sb", slope)
-        gain_sb = load_by_row("gain_sb", gain)
+        wt_rows = held("wt_rows", [P, H // 4], I32)
+        nc.sync.dma_start(out=wt_rows[16:32, :], in_=wt_scales[0].bitcast(I32).rearrange("(q r) c -> r q c", r=4))
+        for rows in (slice(0, 16), slice(32, 64), slice(64, P)):
+            nc.gpsimd.memset(wt_rows[rows, :], 0)
+        tab_raw = [load_words("tab0", tab_words[0].rearrange("p t i -> p (t i)"))]
+        load_w1(0, 0)
+        tab_raw.append(load_words("tab1", tab_words[1].rearrange("p t i -> p (t i)")))
         list2 = keep.tile([P, M // 16], U16, name="list2")
         nc.sync.dma_start(list2[:], offs2)
-        load_first_pass((2, 3))
-        load_plane(tab_plane, tab_scales, nc.sync)
-        load_w1(0, 0, 2)
-        tab_raw.append(load_words("tab1", tab_words[1].rearrange("p t i -> p (t i)")))
+        v_rows = held("v_rows", [P, S], U8)
+        nc.vector.tensor_copy(out=v_rows[:], in_=tab_rows[:].bitcast(U8).indirect(list1[:]))
+        v_plane = held("v_plane", [P, S], U8)
+        for q in range(4):
+            nc.sync.dma_start(
+                out=v_plane[:].bitcast(I32)[32 * q : 32 * q + 8, :], in_=v_rows[:].bitcast(I32)[q:32:4, :]
+            )
         load_w1(0, 1, 2)
-        wt_raw = load_words("wt_raw", wt_words[0])
-        load_plane(wt_plane, wt_scales, nc.sync)
         wgt_sb = held("wgt_sb", [P, M], F32)
         nc.sync.dma_start(out=wgt_sb[:], in_=wgt)
+        wt_raw = load_words("wt_raw", wt_words[0])
+        wt_dealt = held("wt_dealt", [P, H], U8)
+        nc.vector.tensor_copy(
+            out=wt_dealt[:].rearrange("p (b i m) -> p b i m", b=2, i=PACK),
+            in_=wt_rows[:].bitcast(U8).rearrange("p (b m i) -> p b i m", b=2, i=PACK),
+        )
         load_w1(1, 0)
         load_w1(1, 1)
-        tgt_raw = load_rows("tgt", tgt)
+        tgt_raw = [load_rows("tgt%d" % u, tgt[:, u * M // 2 : (u + 1) * M // 2]) for u in range(2)]
+        wt_scale = held("wt_scale", [P, H], U8)
+        for q in range(4):
+            nc.sync.dma_start(
+                out=wt_scale[:].bitcast(I32)[32 * q : 32 * q + 4, :], in_=wt_dealt[:].bitcast(I32)[16 + q : 32 : 4, :]
+            )
+        slope_sb = load_by_row("slope_sb", slope)
+        gain_sb = load_by_row("gain_sb", gain)
         wo_plane = held("wo_plane", [P, N // 4], I32)
         load_plane(wo_plane, wo_scales, nc.sync)
         wo_codes = [load_words("wo%d" % b, wo_words[b].rearrange("p c i -> p (c i)")) for b in range(2)]
@@ -152,7 +172,7 @@ def tile_list_ontology_facet_match_kernel(
         v_codes = {}
 
         def gather_words(a, pieces):
-            v_codes[a] = held("v%d" % a, [P, S], U32, tag=("v0", "w1_001")[a])
+            v_codes[a] = held("v%d" % a, [P, S], U32)
             width = S // pieces
             for first in range(0, S, width):
                 nc.vector.tensor_copy(
@@ -185,8 +205,6 @@ def tile_list_ontology_facet_match_kernel(
             w1_q[b, a] = quantise("w1q%d%d" % (b, a), w1_grouped[b, a], widths)
 
         gather_words(0, 1)
-        v_plane = held("v_plane", [P, S], U8)
-        nc.vector.tensor_copy(out=v_plane[:], in_=tab_plane[:].bitcast(U8).indirect(list1[:]))
         round_w1(0, 0)
         quantise_w1(0, 0, (PASS,))
         gather_words(1, 1)
@@ -195,23 +213,35 @@ def tile_list_ontology_facet_match_kernel(
 
         h_sb = {}
 
-        def make_h(b, i, first_bank):
-            h_sb[b, i] = held("h%d%d" % (b, i), [P, S], F32, tag=H_TAGS.get((b, i)))
+        h_banks = {}
+
+        def h_pass(b, i, s, a):
+            codes, plane = w1_q[b, a]
+            cols = slice(BANK * s, BANK * (s + 1))
+            nc.tensor.matmul_mx(
+                out=h_banks[b, i, s][:],
+                lhsT=codes[:, P * i : P * (i + 1)].bitcast(E4M3),
+                lhsT_scale=plane[:, P * i : P * (i + 1)],
+                rhs=v_codes[a][:, cols].bitcast(E4M3),
+                rhs_scale=v_plane[4 * a :, cols],
+                start=(a == b),
+                stop=(a != b),
+            )
+
+        def open_h(b, i, first_bank):
             for s in range(2):
-                bank = bank_tile(first_bank + s, [P, BANK])
-                cols = slice(BANK * s, BANK * (s + 1))
-                for a in (b, 1 - b):
-                    codes, plane = w1_q[b, a]
-                    nc.tensor.matmul_mx(
-                        out=bank[:],
-                        lhsT=codes[:, P * i : P * (i + 1)].bitcast(E4M3),
-                        lhsT_scale=plane[:, P * i : P * (i + 1)],
-                        rhs=v_codes[a][:, cols].bitcast(E4M3),
-                        rhs_scale=v_plane[4 * a :, cols],
-                        start=(a == b),
-                        stop=(a != b),
-                    )
-                nc.scalar.copy(out=h_sb[b, i][:, cols], in_=bank[:])
+                h_banks[b, i, s] = bank_tile(first_bank + s, [P, BANK])
+                h_pass(b, i, s, b)
+
+        def make_h(b, i, first_bank):
+            h_sb[b, i] = held("h%d%d" % (b, i), [P, S], F32)
+            for s in range(2):
+                if (b, i, s) not in h_banks:
+                    h_banks[b, i, s] = bank_tile(first_bank + s, [P, BANK])
+                    h_pass(b, i, s, b)
+                h_pass(b, i, s, 1 - b)
+                engine = "vector" if (b, i, s) == (0, 0, 1) else "scalar"
+                copy_on(engine, h_sb[b, i][:, BANK * s : BANK * (s + 1)], h_banks[b, i, s][:])
 
         x_first = {}
         x_pair = {}
@@ -314,16 +344,13 @@ def tile_list_ontology_facet_match_kernel(
                     out=out.rearrange("(c p) m -> p c m", p=P)[:, c0 : c0 + count, m0 : m0 + width], in_=staged[:]
                 )
 
+        open_h(0, 0, 0)
+        open_h(0, 1, 2)
         make_h(0, 0, 0)
-        wt_codes = held("wt_codes", [P, H], U16, tag="w1_grouped01")
+        wt_codes = held("wt_codes", [P, H], U16)
         nc.vector.tensor_copy(
             out=wt_codes[:].rearrange("p (b i m) -> p b i m", b=2, i=PACK),
             in_=wt_raw[:].bitcast(U16).rearrange("p (b m i) -> p b i m", b=2, i=PACK),
-        )
-        wt_scale = held("wt_scale", [P, H], U8, tag="w1_011")
-        nc.vector.tensor_copy(
-            out=wt_scale[:].rearrange("p (b i m) -> p b i m", b=2, i=PACK),
-            in_=wt_plane[:].bitcast(U8).rearrange("p (b m i) -> p b i m", b=2, i=PACK),
         )
         half = M // 2
         tgt_grouped = {}
@@ -339,7 +366,7 @@ def tile_list_ontology_facet_match_kernel(
             copy_on(
                 engine,
                 tgt_grouped[u][:].rearrange("p (c i j) -> p c j i", i=4, j=PACK),
-                tgt_raw[:, :, half * u : half * (u + 1)].rearrange("p j (c i) -> p c j i", i=4),
+                tgt_raw[u][:].rearrange("p j (c i) -> p c j i", i=4),
             )
 
         pick(0, 0)

@@ -25,7 +25,7 @@ G_TAGS = {(1, 1): "h01"}
 PLACES = {
     "w1_110": 0, "w1q10_codes": 0, "tgt_grouped0": 2048, "e0": 0,
     "tab1": 8128, "tgt1": 8192, "tgt0": 12288, "h10": 12288,
-    "w1_000": 24448, "w1_100": 32576, "h03": 32832,
+    "w1_000": 24448, "wt_dealt": 24448, "w1_100": 32576, "h03": 32832,
     "tab0": 40768, "wgt_sb": 40768, "wt_raw": 42816,
     "w1_grouped01": 57344, "wt_codes": 57344,
     "w1_grouped00": 61440, "v1": 61440,
@@ -34,7 +34,7 @@ PLACES = {
 }
 OUT_BANKS = ((0, 1), (2, 3), (6, 7), (4, 5))
 W1_PIECES = {
-    (0, 0): ((320, "scalar"), (192, "vector")),
+    (0, 0): ((176, "scalar"), (336, "vector")),
     (0, 1): ((256, "scalar"), (96, "scalar"), (160, "vector")),
     (1, 0): ((512, "scalar"),),
     (1, 1): ((512, "vector"),),
@@ -96,32 +96,34 @@ def tile_list_ontology_facet_match_kernel(
             w1_raw[b, a] = PASS
 
         tab_rows = held("tab_rows", [P, T // 4], I32)
-        for a in range(2):
-            nc.sync.dma_start(
-                out=tab_rows[16 * a : 16 * (a + 1), :],
-                in_=tab_scales[a].bitcast(I32).rearrange("(q r) t -> r q t", r=4),
-            )
+        nc.sync.dma_start(out=tab_rows[0:32, :], in_=tab_scales.bitcast(I32).rearrange("a g t -> (a g) t"))
         nc.vector.memset(tab_rows[32:64, :], 0)
         nc.vector.memset(tab_rows[64:, :], 0)
         list1 = keep.tile([P, S // 16], U16, name="list1")
         nc.sync.dma_start(list1[:], offs)
+        tab_raw = [load_words("tab0", tab_words[0].rearrange("p t i -> p (t i)"))]
+        load_w1(0, 0)
         wt_rows = held("wt_rows", [P, H // 4], I32)
         nc.sync.dma_start(out=wt_rows[16:32, :], in_=wt_scales[0].bitcast(I32).rearrange("(q r) c -> r q c", r=4))
         for rows in (slice(0, 16), slice(32, 64), slice(64, P)):
             nc.gpsimd.memset(wt_rows[rows, :], 0)
-        tab_raw = [load_words("tab0", tab_words[0].rearrange("p t i -> p (t i)"))]
-        load_w1(0, 0)
         tab_raw.append(load_words("tab1", tab_words[1].rearrange("p t i -> p (t i)")))
         list2 = keep.tile([P, M // 16], U16, name="list2")
         nc.sync.dma_start(list2[:], offs2)
         v_rows = held("v_rows", [P, S], U8)
         nc.vector.tensor_copy(out=v_rows[:], in_=tab_rows[:].bitcast(U8).indirect(list1[:]))
-        v_plane = held("v_plane", [P, S], U8)
-        for q in range(4):
-            nc.sync.dma_start(
-                out=v_plane[:].bitcast(I32)[32 * q : 32 * q + 8, :], in_=v_rows[:].bitcast(I32)[q:32:4, :]
-            )
+        v_plane = [held("v_plane%d" % a, [P, S], U8) for a in range(2)]
+
+        def place_rows(a):
+            for q in range(4):
+                nc.sync.dma_start(
+                    out=v_plane[a][:].bitcast(I32)[32 * q + 4 * a : 32 * q + 4 * a + 4, :],
+                    in_=v_rows[:].bitcast(I32)[16 * a + 4 * q : 16 * a + 4 * q + 4, :],
+                )
+
+        place_rows(0)
         load_w1(0, 1, 2)
+        place_rows(1)
         wgt_sb = held("wgt_sb", [P, M], F32)
         nc.sync.dma_start(out=wgt_sb[:], in_=wgt)
         wt_raw = load_words("wt_raw", wt_words[0])
@@ -223,7 +225,7 @@ def tile_list_ontology_facet_match_kernel(
                 lhsT=codes[:, P * i : P * (i + 1)].bitcast(E4M3),
                 lhsT_scale=plane[:, P * i : P * (i + 1)],
                 rhs=v_codes[a][:, cols].bitcast(E4M3),
-                rhs_scale=v_plane[4 * a :, cols],
+                rhs_scale=v_plane[a][4 * a :, cols],
                 start=(a == b),
                 stop=(a != b),
             )
@@ -240,7 +242,7 @@ def tile_list_ontology_facet_match_kernel(
                     h_banks[b, i, s] = bank_tile(first_bank + s, [P, BANK])
                     h_pass(b, i, s, b)
                 h_pass(b, i, s, 1 - b)
-                engine = "vector" if (b, i, s) == (0, 0, 1) else "scalar"
+                engine = "vector" if (b, i, s) == (0, 0, 0) else "scalar"
                 copy_on(engine, h_sb[b, i][:, BANK * s : BANK * (s + 1)], h_banks[b, i, s][:])
 
         x_first = {}

@@ -104,7 +104,7 @@ def tile_list_ontology_facet_match_kernel(
         tab_raw = [load_words("tab0", tab_words[0].rearrange("p t i -> p (t i)"))]
         load_w1(0, 0)
         wt_rows = held("wt_rows", [P, H // 4], I32)
-        nc.sync.dma_start(out=wt_rows[16:32, :], in_=wt_scales[0].bitcast(I32).rearrange("(q r) c -> r q c", r=4))
+        nc.sync.dma_start(out=wt_rows[16:32, :], in_=wt_scales[0].bitcast(I32))
         for rows in (slice(0, 16), slice(32, 64), slice(64, P)):
             nc.gpsimd.memset(wt_rows[rows, :], 0)
         tab_raw.append(load_words("tab1", tab_words[1].rearrange("p t i -> p (t i)")))
@@ -138,7 +138,8 @@ def tile_list_ontology_facet_match_kernel(
         wt_scale = held("wt_scale", [P, H], U8)
         for q in range(4):
             nc.sync.dma_start(
-                out=wt_scale[:].bitcast(I32)[32 * q : 32 * q + 4, :], in_=wt_dealt[:].bitcast(I32)[16 + q : 32 : 4, :]
+                out=wt_scale[:].bitcast(I32)[32 * q : 32 * q + 4, :],
+                in_=wt_dealt[:].bitcast(I32)[16 + 4 * q : 20 + 4 * q, :],
             )
         slope_sb = load_by_row("slope_sb", slope)
         gain_sb = load_by_row("gain_sb", gain)
@@ -226,22 +227,22 @@ def tile_list_ontology_facet_match_kernel(
                 lhsT_scale=plane[:, P * i : P * (i + 1)],
                 rhs=v_codes[a][:, cols].bitcast(E4M3),
                 rhs_scale=v_plane[a][4 * a :, cols],
-                start=(a == b),
-                stop=(a != b),
+                start=(a == 0),
+                stop=(a == 1),
             )
 
         def open_h(b, i, first_bank):
             for s in range(2):
                 h_banks[b, i, s] = bank_tile(first_bank + s, [P, BANK])
-                h_pass(b, i, s, b)
+                h_pass(b, i, s, 0)
 
         def make_h(b, i, first_bank):
             h_sb[b, i] = held("h%d%d" % (b, i), [P, S], F32)
             for s in range(2):
                 if (b, i, s) not in h_banks:
                     h_banks[b, i, s] = bank_tile(first_bank + s, [P, BANK])
-                    h_pass(b, i, s, b)
-                h_pass(b, i, s, 1 - b)
+                    h_pass(b, i, s, 0)
+                h_pass(b, i, s, 1)
                 engine = "vector" if (b, i, s) == (0, 0, 0) else "scalar"
                 copy_on(engine, h_sb[b, i][:, BANK * s : BANK * (s + 1)], h_banks[b, i, s][:])
 
@@ -299,52 +300,70 @@ def tile_list_ontology_facet_match_kernel(
 
         z_q = {}
 
-        def make_z(b, m0, width, tag=None):
-            name = "z%d_%d" % (b, m0)
-            z_sb = held(name, [P, width * PACK], BF16, tag=tag)
-            if b == 0:
-                nc.vector.tensor_copy(
-                    out=z_sb[:].rearrange("p (c i t) -> p c t i", i=4, t=PACK),
-                    in_=z_planes[:, :, m0 : m0 + width].rearrange("p t (c i) -> p c t i", i=4),
-                )
-            else:
-                weigh(b, m0, width, z_sb)
-            codes, plane = quantise(name, z_sb, (width,))
-            for first in range(0, width, P):
-                z_q[b, m0 + first] = (codes, plane, first)
+        z_sb = {}
 
-        def weigh(b, m0, width, z_sb):
+        def z_part(step, b):
+            parts = [c for c in (1, 0) if 0 <= step - c < M // P]
+            if step not in z_sb:
+                tag = "sq1_%d" % (P * (step - 2)) if 1 < step < M // P else None
+                z_sb[step] = held("z%d" % step, [P, len(parts) * P * PACK], BF16, tag=tag)
+            first = parts.index(b) * P * PACK
+            return z_sb[step][:, first : first + P * PACK]
+
+        def weave(m0):
+            nc.vector.tensor_copy(
+                out=z_part(m0 // P, 0).rearrange("p (c i t) -> p c t i", i=4, t=PACK),
+                in_=z_planes[:, :, m0 : m0 + P].rearrange("p t (c i) -> p c t i", i=4),
+            )
+
+        def quantise_z(step):
+            parts = [c for c in (1, 0) if 0 <= step - c < M // P]
+            codes, plane = quantise("z%d" % step, z_sb[step], (len(parts) * P,))
+            for n, b in enumerate(parts):
+                z_q[b, P * (step - b)] = (codes, plane, P * n)
+
+        def weigh(b, m0, width):
             nc.vector.tensor_tensor(
-                out=z_sb[:].rearrange("p (c i t) -> p c t i", i=4, t=PACK),
+                out=z_part(m0 // P + 1, 1).rearrange("p (c i t) -> p c t i", i=4, t=PACK),
                 in0=e_sb[b][:, :, m0 : m0 + width].rearrange("p t (c i) -> p c t i", i=4),
                 in1=gain_sb[:, b, :].unsqueeze(1).unsqueeze(3).to_broadcast([P, width // 4, PACK, 4]),
                 op=ALU.mult,
             )
 
-        def make_out(m0, width, banks):
-            count = N // P // len(banks)
-            for turn, number in enumerate(banks):
-                c0 = turn * count
-                bank = bank_tile(number, [P, count, width])
-                for b in range(2):
-                    codes, plane, first = z_q[b, m0]
-                    for n in range(count):
-                        cols = slice(P * (c0 + n), P * (c0 + n + 1))
-                        nc.tensor.matmul_mx(
-                            out=bank[:, n, :],
-                            lhsT=wo_codes[b][:, cols].bitcast(E4M3),
-                            lhsT_scale=wo_plane[:].bitcast(U8)[4 * b :, cols],
-                            rhs=codes[:, first : first + width].bitcast(E4M3),
-                            rhs_scale=plane[:, first : first + width],
-                            start=(b == 0 and n == 0),
-                            stop=(b == 1 and n == count - 1),
-                        )
-                staged = held("staged%d_%d" % (m0, c0), [P, count, width], F32)
-                last = m0 + width == M and turn == 1
-                copy_on("vector" if last else "scalar", staged[:], bank[:])
-                nc.sync.dma_start(
-                    out=out.rearrange("(c p) m -> p c m", p=P)[:, c0 : c0 + count, m0 : m0 + width], in_=staged[:]
-                )
+        out_banks = {}
+
+        def make_out(m0, width, numbers):
+            count = N // P // len(numbers)
+            banks = [bank_tile(number, [P, count, width]) for number in numbers]
+
+            def out_passes(turn, b):
+                codes, plane, first = z_q[b, m0]
+                for n in range(count):
+                    cols = slice(P * (turn * count + n), P * (turn * count + n + 1))
+                    nc.tensor.matmul_mx(
+                        out=banks[turn][:, n, :],
+                        lhsT=wo_codes[b][:, cols].bitcast(E4M3),
+                        lhsT_scale=wo_plane[:].bitcast(U8)[4 * b :, cols],
+                        rhs=codes[:, first : first + width].bitcast(E4M3),
+                        rhs_scale=plane[:, first : first + width],
+                        start=(b == 0 and n == 0),
+                        stop=(b == 1 and n == count - 1),
+                    )
+
+            for b in range(2):
+                for turn in range(len(banks)):
+                    out_passes(turn, b)
+            out_banks[m0] = banks
+
+        def store_out(m0, turn, engine):
+            bank = out_banks[m0][turn]
+            count, width = N // P // 2, P
+            c0 = turn * count
+            staged = held("staged%d_%d" % (m0, c0), [P, count, width], F32)
+            copy_on(engine, staged[:], bank[:])
+            nc.sync.dma_start(
+                out=out.rearrange("(c p) m -> p c m", p=P)[:, c0 : c0 + count, m0 : m0 + width], in_=staged[:]
+            )
 
         open_h(0, 0, 0)
         open_h(0, 1, 2)
@@ -380,7 +399,7 @@ def tile_list_ontology_facet_match_kernel(
         round_w1(1, 1)
         prepared = [start_quantise("w1q1%d" % a, PASS) for a in range(2)]
         for first, width in ((0, P), (P, P), (2 * P, 2 * P)):
-            for a in (1, 0):
+            for a in (0, 1):
                 quantise_part(prepared[a], w1_grouped[1, a], first, width)
         for a in range(2):
             w1_q[1, a] = prepared[a]
@@ -390,6 +409,7 @@ def tile_list_ontology_facet_match_kernel(
         quantise_tgt(0)
         quantise_tgt(1)
         pick(0, 3)
+        open_h(1, 0, 0)
         make_h(1, 0, 0)
         pick(1, 0)
         make_h(1, 1, 2)
@@ -417,16 +437,22 @@ def tile_list_ontology_facet_match_kernel(
                 op1=ALU.add,
             )
         subtract_pair(1, 1, 5)
-        make_z(0, 0, P)
+        weave(0)
+        quantise_z(0)
         for u in range(2):
             squares = held("sq1_pair%d" % u, [P, 2, half], F32)
             gaussian(1, 0, 2, slice(half * u, half * (u + 1)), squares[:])
             for m0 in range(half * u, half * (u + 1), P):
                 squares = held("sq1_%d" % m0, [P, 2, P], F32)
                 gaussian(1, 2, 2, slice(m0, m0 + P), squares[:])
-        make_z(0, P, P)
         for m0 in range(0, M, P):
-            if m0 > P:
-                make_z(0, m0, P, tag="sq1_%d" % (m0 - P))
-            make_z(1, m0, P)
+            if m0 + P < M:
+                weave(m0 + P)
+            weigh(1, m0, P)
+            quantise_z(m0 // P + 1)
             make_out(m0, P, OUT_BANKS[m0 // P])
+            if m0 == M - P:
+                store_out(m0 - P, 1, "vector")
+            store_out(m0, 0, "scalar")
+            if m0 != M - 2 * P:
+                store_out(m0, 1, "vector" if m0 == M - P else "scalar")

@@ -299,64 +299,70 @@ def tile_list_ontology_facet_match_kernel(
                 )
 
         z_q = {}
-
+        z_planes = {}
         z_sb = {}
 
-        def z_part(step, b):
-            parts = [c for c in (1, 0) if 0 <= step - c < M // P]
-            if step not in z_sb:
-                tag = "sq1_%d" % (P * (step - 2)) if 1 < step < M // P else None
-                z_sb[step] = held("z%d" % step, [P, len(parts) * P * PACK], BF16, tag=tag)
-            first = parts.index(b) * P * PACK
-            return z_sb[step][:, first : first + P * PACK]
-
-        def weave(m0):
-            nc.vector.tensor_copy(
-                out=z_part(m0 // P, 0).rearrange("p (c i t) -> p c t i", i=4, t=PACK),
-                in_=z_planes[:, :, m0 : m0 + P].rearrange("p t (c i) -> p c t i", i=4),
+        def gain_first(u, i):
+            cols = slice(half * u, half * (u + 1))
+            if u not in z_planes:
+                z_planes[u] = held("z_planes%d" % u, [P, PACK, half], BF16, tag=("h13", "v0")[u])
+            nc.gpsimd.tensor_scalar(
+                out=z_planes[u][:, i, :],
+                in0=e_sb[0][:, i, cols],
+                scalar1=gain_sb[:, 0, i : i + 1],
+                scalar2=0.0,
+                op0=ALU.mult,
+                op1=ALU.add,
             )
 
-        def quantise_z(step):
-            parts = [c for c in (1, 0) if 0 <= step - c < M // P]
-            codes, plane = quantise("z%d" % step, z_sb[step], (len(parts) * P,))
-            for n, b in enumerate(parts):
-                z_q[b, P * (step - b)] = (codes, plane, P * n)
+        def weave(u):
+            z_sb[0, u] = held("z0_%d" % u, [P, half * PACK], BF16, tag=(None, "sq1_%d" % P)[u])
+            nc.vector.tensor_copy(
+                out=z_sb[0, u][:].rearrange("p (c i t) -> p c t i", i=4, t=PACK),
+                in_=z_planes[u][:].rearrange("p t (c i) -> p c t i", i=4),
+            )
 
-        def weigh(b, m0, width):
+        def quantise_first(u):
+            codes = held("z0_codes%d" % u, [P, half], U32, tag="sq1_%d" % (half * u))
+            plane = held("z0_plane%d" % u, [P, half], U8)
+            quantise_part((codes, plane), z_sb[0, u], 0, half)
+            for n in range(2):
+                z_q[0, half * u + P * n] = (codes, plane, P * n)
+
+        def quantise_second(m0):
+            codes, plane = quantise("z1_%d" % m0, z_sb[1, m0], (P,))
+            z_q[1, m0] = (codes, plane, 0)
+
+        def weigh(m0):
+            z_sb[1, m0] = held("z1_%d" % m0, [P, P * PACK], BF16)
             nc.vector.tensor_tensor(
-                out=z_part(m0 // P + 1, 1).rearrange("p (c i t) -> p c t i", i=4, t=PACK),
-                in0=e_sb[b][:, :, m0 : m0 + width].rearrange("p t (c i) -> p c t i", i=4),
-                in1=gain_sb[:, b, :].unsqueeze(1).unsqueeze(3).to_broadcast([P, width // 4, PACK, 4]),
+                out=z_sb[1, m0][:].rearrange("p (c i t) -> p c t i", i=4, t=PACK),
+                in0=e_sb[1][:, :, m0 : m0 + P].rearrange("p t (c i) -> p c t i", i=4),
+                in1=gain_sb[:, 1, :].unsqueeze(1).unsqueeze(3).to_broadcast([P, P // 4, PACK, 4]),
                 op=ALU.mult,
             )
 
         out_banks = {}
 
-        def make_out(m0, width, numbers):
-            count = N // P // len(numbers)
-            banks = [bank_tile(number, [P, count, width]) for number in numbers]
-
-            def out_passes(turn, b):
-                codes, plane, first = z_q[b, m0]
-                for n in range(count):
-                    cols = slice(P * (turn * count + n), P * (turn * count + n + 1))
-                    nc.tensor.matmul_mx(
-                        out=banks[turn][:, n, :],
-                        lhsT=wo_codes[b][:, cols].bitcast(E4M3),
-                        lhsT_scale=wo_plane[:].bitcast(U8)[4 * b :, cols],
-                        rhs=codes[:, first : first + width].bitcast(E4M3),
-                        rhs_scale=plane[:, first : first + width],
-                        start=(b == 0 and n == 0),
-                        stop=(b == 1 and n == count - 1),
-                    )
-
-            for b in range(2):
-                for turn in range(len(banks)):
-                    out_passes(turn, b)
-            out_banks[m0] = banks
+        def out_passes(m0, turn, b):
+            count = N // P // 2
+            if b == 0:
+                out_banks[m0, turn] = bank_tile(OUT_BANKS[m0 // P][turn], [P, count, P])
+            codes, plane, first = z_q[b, m0]
+            for n in range(count):
+                cols = slice(P * (turn * count + n), P * (turn * count + n + 1))
+                nc.tensor.matmul_mx(
+                    out=out_banks[m0, turn][:, n, :],
+                    lhsT=wo_codes[b][:, cols].bitcast(E4M3),
+                    lhsT_scale=wo_plane[:].bitcast(U8)[4 * b :, cols],
+                    rhs=codes[:, first : first + P].bitcast(E4M3),
+                    rhs_scale=plane[:, first : first + P],
+                    start=(b == 0 and n == 0),
+                    stop=(b == 1 and n == count - 1),
+                )
 
         def store_out(m0, turn, engine):
-            bank = out_banks[m0][turn]
+            bank = out_banks[m0, turn]
             count, width = N // P // 2, P
             c0 = turn * count
             staged = held("staged%d_%d" % (m0, c0), [P, count, width], F32)
@@ -418,41 +424,65 @@ def tile_list_ontology_facet_match_kernel(
         make_h(1, 3, 4)
         subtract(0, 0)
         subtract(1, 1)
-        pick(1, 2)
         subtract(2, 2)
+        pick(1, 2)
         subtract(3, 3)
-        subtract_pair(0, 0, 6)
         pick(1, 3)
-        subtract_pair(0, 1, 7)
+        subtract_pair(0, 0, 6)
         subtract_pair(1, 0, 4)
-        z_planes = held("z_planes", [P, PACK, M], BF16, tag="h12")
+        subtract_pair(0, 1, 7)
+        subtract_pair(1, 1, 5)
         for i in range(PACK):
             gaussian(0, i, 1, slice(0, M), sq_first[:, i : i + 1, :])
-            nc.gpsimd.tensor_scalar(
-                out=z_planes[:, i, :],
-                in0=e_sb[0][:, i, :],
-                scalar1=gain_sb[:, 0, i : i + 1],
-                scalar2=0.0,
-                op0=ALU.mult,
-                op1=ALU.add,
-            )
-        subtract_pair(1, 1, 5)
-        weave(0)
-        quantise_z(0)
-        for u in range(2):
+            gain_first(0, i)
+        for i in range(PACK):
+            gain_first(1, i)
+
+        def gaussian_pair(u):
             squares = held("sq1_pair%d" % u, [P, 2, half], F32)
             gaussian(1, 0, 2, slice(half * u, half * (u + 1)), squares[:])
-            for m0 in range(half * u, half * (u + 1), P):
-                squares = held("sq1_%d" % m0, [P, 2, P], F32)
-                gaussian(1, 2, 2, slice(m0, m0 + P), squares[:])
-        for m0 in range(0, M, P):
-            if m0 + P < M:
-                weave(m0 + P)
-            weigh(1, m0, P)
-            quantise_z(m0 // P + 1)
-            make_out(m0, P, OUT_BANKS[m0 // P])
-            if m0 == M - P:
-                store_out(m0 - P, 1, "vector")
-            store_out(m0, 0, "scalar")
-            if m0 != M - 2 * P:
-                store_out(m0, 1, "vector" if m0 == M - P else "scalar")
+
+        def gaussian_range(m0):
+            squares = held("sq1_%d" % m0, [P, 2, P], F32)
+            gaussian(1, 2, 2, slice(m0, m0 + P), squares[:])
+
+        weave(0)
+        gaussian_pair(0)
+        gaussian_range(0)
+        gaussian_range(P)
+        weigh(0)
+        quantise_first(0)
+        quantise_second(0)
+        for turn in range(2):
+            for b in range(2):
+                out_passes(0, turn, b)
+        for turn in range(2):
+            out_passes(P, turn, 0)
+        gaussian_pair(1)
+        gaussian_range(2 * P)
+        weigh(P)
+        weave(1)
+        quantise_second(P)
+        for turn in range(2):
+            out_passes(P, turn, 1)
+        store_out(0, 0, "scalar")
+        store_out(0, 1, "scalar")
+        gaussian_range(3 * P)
+        weigh(2 * P)
+        quantise_first(1)
+        quantise_second(2 * P)
+        for turn in range(2):
+            for b in range(2):
+                out_passes(2 * P, turn, b)
+        for turn in range(2):
+            out_passes(3 * P, turn, 0)
+        store_out(P, 0, "scalar")
+        store_out(P, 1, "scalar")
+        weigh(3 * P)
+        quantise_second(3 * P)
+        for turn in range(2):
+            out_passes(3 * P, turn, 1)
+        store_out(2 * P, 0, "scalar")
+        store_out(2 * P, 1, "vector")
+        store_out(3 * P, 0, "scalar")
+        store_out(3 * P, 1, "vector")

@@ -290,25 +290,31 @@ def tile_list_ontology_facet_match_kernel(
         sq_first = held("sq0", [P, PACK, M], F32, tag="v0")
         e_sb = [held("e%d" % b, [P, PACK, M], F32) for b in range(2)]
 
-        def gaussian(b, first, count, cols, squares):
-            nc.scalar.activation(out=squares, in_=d_sb[b][:, first : first + count, cols], func=ACT.Square)
+        squares = {}
+
+        def square(name, b, first, count, cols):
+            if b == 0:
+                target = sq_first[:, first : first + count, :]
+            else:
+                target = held(name, [P, count, cols.stop - cols.start], F32)[:]
+            nc.scalar.activation(out=target, in_=d_sb[b][:, first : first + count, cols], func=ACT.Square)
+            squares[name] = (target, b, first, count, cols)
+
+        def exponential(name):
+            source, b, first, count, cols = squares[name]
             for n in range(count):
                 i = first + n
                 nc.scalar.activation(
-                    out=e_sb[b][:, i, cols], in_=squares[:, n, :], func=ACT.Exp, scale=slope_sb[:, b, i : i + 1]
+                    out=e_sb[b][:, i, cols], in_=source[:, n, :], func=ACT.Exp, scale=slope_sb[:, b, i : i + 1]
                 )
 
         z_q = {}
-        z_planes = {}
         z_sb = {}
 
-        def gain_first(u, i):
-            cols = slice(half * u, half * (u + 1))
-            if u not in z_planes:
-                z_planes[u] = held("z_planes%d" % u, [P, PACK, half], BF16, tag=("h13", "v0")[u])
+        def gain_first(i):
             nc.gpsimd.tensor_scalar(
-                out=z_planes[u][:, i, :],
-                in0=e_sb[0][:, i, cols],
+                out=z_planes[:, i, :],
+                in0=e_sb[0][:, i, :],
                 scalar1=gain_sb[:, 0, i : i + 1],
                 scalar2=0.0,
                 op0=ALU.mult,
@@ -319,7 +325,7 @@ def tile_list_ontology_facet_match_kernel(
             z_sb[0, u] = held("z0_%d" % u, [P, half * PACK], BF16, tag=(None, "sq1_%d" % P)[u])
             nc.vector.tensor_copy(
                 out=z_sb[0, u][:].rearrange("p (c i t) -> p c t i", i=4, t=PACK),
-                in_=z_planes[u][:].rearrange("p t (c i) -> p c t i", i=4),
+                in_=z_planes[:, :, half * u : half * (u + 1)].rearrange("p t (c i) -> p c t i", i=4),
             )
 
         def quantise_first(u):
@@ -432,24 +438,33 @@ def tile_list_ontology_facet_match_kernel(
         subtract_pair(1, 0, 4)
         subtract_pair(0, 1, 7)
         subtract_pair(1, 1, 5)
+        z_planes = held("z_planes", [P, PACK, M], BF16, tag="h12")
+
+        def square_pair(u):
+            square("sq1_pair%d" % u, 1, 0, 2, slice(half * u, half * (u + 1)))
+
+        def square_range(m0):
+            square("sq1_%d" % m0, 1, 2, 2, slice(m0, m0 + P))
+
+        square("sq0_0", 0, 0, 1, slice(0, M))
         for i in range(PACK):
-            gaussian(0, i, 1, slice(0, M), sq_first[:, i : i + 1, :])
-            gain_first(0, i)
-        for i in range(PACK):
-            gain_first(1, i)
-
-        def gaussian_pair(u):
-            squares = held("sq1_pair%d" % u, [P, 2, half], F32)
-            gaussian(1, 0, 2, slice(half * u, half * (u + 1)), squares[:])
-
-        def gaussian_range(m0):
-            squares = held("sq1_%d" % m0, [P, 2, P], F32)
-            gaussian(1, 2, 2, slice(m0, m0 + P), squares[:])
-
+            if i + 1 < PACK:
+                square("sq0_%d" % (i + 1), 0, i + 1, 1, slice(0, M))
+            exponential("sq0_%d" % i)
+            gain_first(i)
         weave(0)
-        gaussian_pair(0)
-        gaussian_range(0)
-        gaussian_range(P)
+        square_pair(0)
+        square_range(0)
+        exponential("sq1_pair0")
+        square_range(P)
+        exponential("sq1_0")
+        square_pair(1)
+        exponential("sq1_%d" % P)
+        square_range(2 * P)
+        exponential("sq1_pair1")
+        square_range(3 * P)
+        exponential("sq1_%d" % (2 * P))
+        exponential("sq1_%d" % (3 * P))
         weigh(0)
         quantise_first(0)
         quantise_second(0)
@@ -458,8 +473,6 @@ def tile_list_ontology_facet_match_kernel(
                 out_passes(0, turn, b)
         for turn in range(2):
             out_passes(P, turn, 0)
-        gaussian_pair(1)
-        gaussian_range(2 * P)
         weigh(P)
         weave(1)
         quantise_second(P)
@@ -467,7 +480,6 @@ def tile_list_ontology_facet_match_kernel(
             out_passes(P, turn, 1)
         store_out(0, 0, "scalar")
         store_out(0, 1, "scalar")
-        gaussian_range(3 * P)
         weigh(2 * P)
         quantise_first(1)
         quantise_second(2 * P)
@@ -483,6 +495,6 @@ def tile_list_ontology_facet_match_kernel(
         for turn in range(2):
             out_passes(3 * P, turn, 1)
         store_out(2 * P, 0, "scalar")
-        store_out(2 * P, 1, "vector")
+        store_out(2 * P, 1, "scalar")
         store_out(3 * P, 0, "scalar")
         store_out(3 * P, 1, "vector")

@@ -438,6 +438,8 @@ def tile_list_ontology_facet_match_kernel(
         subtract_pair(1, 0, 4)
         subtract_pair(0, 1, 7)
         subtract_pair(1, 1, 5)
+        for number in (6, 4, 7, 5, 5):
+            target_product(bank_tile(number, [P, BANK])[:], 0, 0, slice(0, M))
         z_planes = held("z_planes", [P, PACK, M], BF16, tag="h12")
 
         def square_pair(u):

@@ -32,7 +32,7 @@ PLACES = {
     "tab_rows": 65536, "w1_010": 67520,
     "wo0": 67584, "wo1": 70656, "wo_plane": 73728, "slope_sb": 74496, "gain_sb": 74560, "wt_scale": 74624,
 }
-OUT_BANKS = ((0, 1), (2, 3), (6, 7), (4, 5))
+OUT_BANKS = ((0, 1), (2, 3), (6, 7), (4, 5, 0))
 W1_PIECES = {
     (0, 0): ((176, "scalar"), (336, "vector")),
     (0, 1): ((256, "scalar"), (96, "scalar"), (160, "vector")),
@@ -218,7 +218,8 @@ def tile_list_ontology_facet_match_kernel(
 
         h_banks = {}
 
-        def h_pass(b, i, s, a):
+        def h_pass(b, i, s, step):
+            a = 1 - step if (b, i) == (0, 2) else step
             codes, plane = w1_q[b, a]
             cols = slice(BANK * s, BANK * (s + 1))
             nc.tensor.matmul_mx(
@@ -227,8 +228,8 @@ def tile_list_ontology_facet_match_kernel(
                 lhsT_scale=plane[:, P * i : P * (i + 1)],
                 rhs=v_codes[a][:, cols].bitcast(E4M3),
                 rhs_scale=v_plane[a][4 * a :, cols],
-                start=(a == 0),
-                stop=(a == 1),
+                start=(step == 0),
+                stop=(step == 1),
             )
 
         def open_h(b, i, first_bank):
@@ -351,7 +352,7 @@ def tile_list_ontology_facet_match_kernel(
         out_banks = {}
 
         def out_passes(m0, turn, b):
-            count = N // P // 2
+            count = N // P // len(OUT_BANKS[m0 // P])
             if b == 0:
                 out_banks[m0, turn] = bank_tile(OUT_BANKS[m0 // P][turn], [P, count, P])
             codes, plane, first = z_q[b, m0]
@@ -369,7 +370,7 @@ def tile_list_ontology_facet_match_kernel(
 
         def store_out(m0, turn, engine):
             bank = out_banks[m0, turn]
-            count, width = N // P // 2, P
+            count, width = N // P // len(OUT_BANKS[m0 // P]), P
             c0 = turn * count
             staged = held("staged%d_%d" % (m0, c0), [P, count, width], F32)
             copy_on(engine, staged[:], bank[:])
@@ -421,7 +422,6 @@ def tile_list_ontology_facet_match_kernel(
         quantise_tgt(0)
         quantise_tgt(1)
         pick(0, 3)
-        open_h(1, 0, 0)
         make_h(1, 0, 0)
         pick(1, 0)
         make_h(1, 1, 2)
@@ -488,15 +488,16 @@ def tile_list_ontology_facet_match_kernel(
         for turn in range(2):
             for b in range(2):
                 out_passes(2 * P, turn, b)
-        for turn in range(2):
+        for turn in range(3):
             out_passes(3 * P, turn, 0)
         store_out(P, 0, "scalar")
         store_out(P, 1, "scalar")
         weigh(3 * P)
         quantise_second(3 * P)
-        for turn in range(2):
+        for turn in range(3):
             out_passes(3 * P, turn, 1)
         store_out(2 * P, 0, "scalar")
-        store_out(2 * P, 1, "scalar")
+        store_out(2 * P, 1, "vector")
         store_out(3 * P, 0, "scalar")
         store_out(3 * P, 1, "vector")
+        store_out(3 * P, 2, "scalar")

@@ -103,9 +103,9 @@ def tile_list_ontology_facet_match_kernel(
         nc.sync.dma_start(list1[:], offs)
         tab_raw = [load_words("tab0", tab_words[0].rearrange("p t i -> p (t i)"))]
         load_w1(0, 0)
-        wt_rows = held("wt_rows", [P, H // 4], I32)
-        nc.sync.dma_start(out=wt_rows[16:32, :], in_=wt_scales[0].bitcast(I32))
-        for rows in (slice(0, 16), slice(32, 64), slice(64, P)):
+        wt_rows = held("wt_rows", [P, PASS // 4], I32)
+        nc.sync.dma_start(out=wt_rows[0:32, :], in_=wt_scales[0].bitcast(I32).rearrange("g (b c) -> (g b) c", b=2))
+        for rows in (slice(32, 64), slice(64, P)):
             nc.gpsimd.memset(wt_rows[rows, :], 0)
         tab_raw.append(load_words("tab1", tab_words[1].rearrange("p t i -> p (t i)")))
         list2 = keep.tile([P, M // 16], U16, name="list2")
@@ -127,10 +127,10 @@ def tile_list_ontology_facet_match_kernel(
         wgt_sb = held("wgt_sb", [P, M], F32)
         nc.sync.dma_start(out=wgt_sb[:], in_=wgt)
         wt_raw = load_words("wt_raw", wt_words[0])
-        wt_dealt = held("wt_dealt", [P, H], U8)
+        wt_dealt = held("wt_dealt", [P, PASS], U8)
         nc.vector.tensor_copy(
-            out=wt_dealt[:].rearrange("p (b i m) -> p b i m", b=2, i=PACK),
-            in_=wt_rows[:].bitcast(U8).rearrange("p (b m i) -> p b i m", b=2, i=PACK),
+            out=wt_dealt[:].rearrange("p (i m) -> p i m", i=PACK),
+            in_=wt_rows[:].bitcast(U8).rearrange("p (m i) -> p i m", i=PACK),
         )
         load_w1(1, 0)
         load_w1(1, 1)
@@ -138,8 +138,8 @@ def tile_list_ontology_facet_match_kernel(
         wt_scale = held("wt_scale", [P, H], U8)
         for q in range(4):
             nc.sync.dma_start(
-                out=wt_scale[:].bitcast(I32)[32 * q : 32 * q + 4, :],
-                in_=wt_dealt[:].bitcast(I32)[16 + 4 * q : 20 + 4 * q, :],
+                out=wt_scale[:].bitcast(I32)[32 * q : 32 * q + 4, :].rearrange("r (b c) -> r b c", b=2),
+                in_=wt_dealt[:].bitcast(I32)[8 * q : 8 * q + 8, :],
             )
         slope_sb = load_by_row("slope_sb", slope)
         gain_sb = load_by_row("gain_sb", gain)
@@ -212,7 +212,7 @@ def tile_list_ontology_facet_match_kernel(
         quantise_w1(0, 0, (PASS,))
         gather_words(1, 1)
         round_w1(0, 1)
-        quantise_w1(0, 1, (P, P, 2 * P))
+        quantise_w1(0, 1, (P, 3 * P))
 
         h_sb = {}
 
@@ -411,7 +411,7 @@ def tile_list_ontology_facet_match_kernel(
         round_w1(1, 0)
         round_w1(1, 1)
         prepared = [start_quantise("w1q1%d" % a, PASS) for a in range(2)]
-        for first, width in ((0, P), (P, P), (2 * P, 2 * P)):
+        for first, width in ((0, P), (P, 3 * P)):
             for a in (0, 1):
                 quantise_part(prepared[a], w1_grouped[1, a], first, width)
         for a in range(2):

@@ -115,7 +115,7 @@ def tile_list_ontology_facet_match_kernel(
         v_plane = [held("v_plane%d" % a, [P, S], U8) for a in range(2)]
 
         def place_rows(a):
-            for q in range(4):
+            for q in (0, 2, 1, 3):
                 nc.sync.dma_start(
                     out=v_plane[a][:].bitcast(I32)[32 * q + 4 * a : 32 * q + 4 * a + 4, :],
                     in_=v_rows[:].bitcast(I32)[16 * a + 4 * q : 16 * a + 4 * q + 4, :],

from contextlib import ExitStack

import concourse.mybir as mybir

K, T, S, M, L, H, N = 1024, 2048, 1024, 512, 512, 1024, 768
FLOPS = 2 * (K * H * S + L * H * M + H * N * M)

F32 = mybir.dt.float32
BF16 = mybir.dt.bfloat16
I32 = mybir.dt.int32
U32 = mybir.dt.uint32
U16 = mybir.dt.uint16
U8 = mybir.dt.uint8
E4M3 = mybir.dt.float8_e4m3fn_x4
E2M1 = mybir.dt.float4_e2m1fn_x4
ALU = mybir.AluOpType
ACT = mybir.ActivationFunctionType

P = 128
PACK = 4
PASS = P * PACK
BANK = 512
X_TAGS = {(0, 3): "w1_grouped10"}
G_TAGS = {(1, 1): "h01"}
PLACES = {
    "w1_110": 0, "w1q10_codes": 0, "tgt_grouped0": 2048, "e0": 0,
    "tab1": 8128, "tgt1": 8192, "tgt0": 12288, "h10": 12288,
    "w1_000": 24448, "wt_dealt": 24448, "w1_100": 32576, "h03": 32832,
    "tab0": 40768, "wgt_sb": 40768, "wt_raw": 42816,
    "w1_grouped01": 57344, "wt_codes": 57344,
    "w1_grouped00": 61440, "v1": 61440,
    "tab_rows": 65536, "w1_010": 67520,
    "wo0": 67584, "wo1": 70656, "wo_plane": 73728, "slope_sb": 74496, "gain_sb": 74560, "wt_scale": 74624,
}
OUT_BANKS = ((0, 1), (2, 3), (6, 7), (4, 5, 0))
W1_PIECES = {
    (0, 0): ((176, "scalar"), (336, "vector")),
    (0, 1): ((256, "scalar"), (96, "scalar"), (160, "vector")),
    (1, 0): ((512, "scalar"),),
    (1, 1): ((512, "vector"),),
}


def tile_list_ontology_facet_match_kernel(
    tc, tab_words, tab_scales, offs, offs2, w1, wgt, tgt, wt_words, wt_scales, slope, gain, wo_words, wo_scales, out
):
    nc = tc.nc
    with ExitStack() as ctx:
        keep = ctx.enter_context(tc.tile_pool(name="keep", bufs=1))
        psum = ctx.enter_context(tc.psum_pool(name="psum", bufs=1))

        shared = ctx.enter_context(tc.tile_pool(name="shared", bufs=1))

        def held(name, shape, dtype, tag=None):
            if name in PLACES:
                return shared.tile(shape, dtype, name=name, align_bytes=64, offset=PLACES[name])
            return keep.tile(shape, dtype, name=name, tag=tag or name, align_bytes=64)

        def bank_tile(number, shape):
            return psum.tile(shape, F32, name="bank%d" % number)

        def load_plane(plane, scales, queue):
            passes = scales.shape[0]
            for q in range(4):
                queue.dma_start(
                    out=plane[32 * q : 32 * q + 4 * passes, :], in_=scales[:, 4 * q : 4 * q + 4, :].bitcast(I32)
                )

        def load_rows(name, src):
            raw = held(name, [P, PACK, src.shape[1]], F32)
            nc.sync.dma_start(out=raw[:], in_=src.rearrange("(p j) c -> p j c", j=PACK))
            return raw

        def load_words(name, src, pieces=1):
            width = src.shape[1] // 4
            words = held(name, [P, width], I32)
            for first in range(0, width, width // pieces):
                cols = slice(first, first + width // pieces)
                nc.sync.dma_start(out=words[:, cols], in_=src.bitcast(I32)[:, cols])
            return words

        def load_by_row(name, vec):
            tile = held(name, [P, 2, PACK], F32)
            nc.sync.dma_start(out=tile[:], in_=vec.rearrange("(b p i) -> p b i", b=2, i=PACK))
            return tile

        w1_raw = {}

        def load_w1(b, a, pieces=1):
            width = PASS // pieces
            raw = held("w1_%d%d0" % (b, a), [P, PACK, PASS], F32)
            block = w1[a * PASS : (a + 1) * PASS, b * PASS : (b + 1) * PASS].rearrange("(p j) c -> p j c", j=PACK)
            for first in range(0, PASS, width):
                nc.sync.dma_start(out=raw[:, :, first : first + width], in_=block[:, :, first : first + width])
            w1_raw[b, a, 0] = raw
            w1_raw[b, a] = PASS

        tab_rows = held("tab_rows", [P, T // 4], I32)
        nc.sync.dma_start(out=tab_rows[0:32, :], in_=tab_scales.bitcast(I32).rearrange("a g t -> (a g) t"))
        nc.vector.memset(tab_rows[32:64, :], 0)
        nc.vector.memset(tab_rows[64:, :], 0)
        list1 = keep.tile([P, S // 16], U16, name="list1")
        nc.sync.dma_start(list1[:], offs)
        tab_raw = [load_words("tab0", tab_words[0].rearrange("p t i -> p (t i)"))]
        load_w1(0, 0)
        wt_rows = held("wt_rows", [P, PASS // 4], I32)
        nc.sync.dma_start(out=wt_rows[0:32, :], in_=wt_scales[0].bitcast(I32).rearrange("g (b c) -> (g b) c", b=2))
        for rows in (slice(32, 64), slice(64, P)):
            nc.gpsimd.memset(wt_rows[rows, :], 0)
        tab_raw.append(load_words("tab1", tab_words[1].rearrange("p t i -> p (t i)")))
        list2 = keep.tile([P, M // 16], U16, name="list2")
        nc.sync.dma_start(list2[:], offs2)
        v_rows = held("v_rows", [P, S], U8)
        nc.vector.tensor_copy(out=v_rows[:], in_=tab_rows[:].bitcast(U8).indirect(list1[:]))
        v_plane = [held("v_plane%d" % a, [P, S], U8) for a in range(2)]

        def place_rows(a):
            for q in (0, 2, 1, 3):
                nc.sync.dma_start(
                    out=v_plane[a][:].bitcast(I32)[32 * q + 4 * a : 32 * q + 4 * a + 4, :],
                    in_=v_rows[:].bitcast(I32)[16 * a + 4 * q : 16 * a + 4 * q + 4, :],
                )

        place_rows(0)
        load_w1(0, 1, 2)
        place_rows(1)
        wgt_sb = held("wgt_sb", [P, M], F32)
        nc.sync.dma_start(out=wgt_sb[:], in_=wgt)
        wt_raw = load_words("wt_raw", wt_words[0])
        wt_dealt = held("wt_dealt", [P, PASS], U8)
        nc.vector.tensor_copy(
            out=wt_dealt[:].rearrange("p (i m) -> p i m", i=PACK),
            in_=wt_rows[:].bitcast(U8).rearrange("p (m i) -> p i m", i=PACK),
        )
        load_w1(1, 0)
        load_w1(1, 1)
        tgt_raw = [load_rows("tgt%d" % u, tgt[:, u * M // 2 : (u + 1) * M // 2]) for u in range(2)]
        wt_scale = held("wt_scale", [P, H], U8)
        for q in range(4):
            nc.sync.dma_start(
                out=wt_scale[:].bitcast(I32)[32 * q : 32 * q + 4, :].rearrange("r (b c) -> r b c", b=2),
                in_=wt_dealt[:].bitcast(I32)[8 * q : 8 * q + 8, :],
            )
        slope_sb = load_by_row("slope_sb", slope)
        gain_sb = load_by_row("gain_sb", gain)
        wo_plane = held("wo_plane", [P, N // 4], I32)
        load_plane(wo_plane, wo_scales, nc.sync)
        wo_codes = [load_words("wo%d" % b, wo_words[b].rearrange("p c i -> p (c i)")) for b in range(2)]

        def copy_on(engine, dst, src):
            if engine == "scalar":
                nc.scalar.copy(out=dst, in_=src)
            else:
                nc.vector.tensor_copy(out=dst, in_=src)

        def start_quantise(name, total):
            return held(name + "_codes", [P, total], U32), held(name + "_plane", [P, total], U8)

        def quantise_part(target, grouped, first, width):
            codes, plane = target
            nc.vector.quantize_mx(
                out=codes[:, first : first + width].bitcast(E4M3),
                scales=plane[:, first : first + width],
                in_=grouped[:, PACK * first : PACK * (first + width)],
            )

        def quantise(name, grouped, widths):
            target = start_quantise(name, sum(widths))
            first = 0
            for width in widths:
                quantise_part(target, grouped, first, width)
                first = first + width
            return target

        v_codes = {}

        def gather_words(a, pieces):
            v_codes[a] = held("v%d" % a, [P, S], U32)
            width = S // pieces
            for first in range(0, S, width):
                nc.vector.tensor_copy(
                    out=v_codes[a][:, first : first + width],
                    in_=tab_raw[a][:].bitcast(U32).indirect(list1[:, first // 16 : (first + width) // 16]),
                )

        w1_grouped = {}
        w1_q = {}

        def round_w1(b, a, only=None):
            if (b, a) not in w1_grouped:
                w1_grouped[b, a] = held("w1_grouped%d%d" % (b, a), [P, PACK * P * PACK], BF16, tag=G_TAGS.get((b, a)))
            view = w1_grouped[b, a][:].rearrange("p (t m j) -> p m j t", t=PACK, j=PACK)
            first = 0
            loaded = w1_raw[b, a]
            for width, engine in W1_PIECES[b, a]:
                if only in (None, engine):
                    local = first % loaded
                    copy_on(
                        engine,
                        view[:, first // PACK : (first + width) // PACK, :, :],
                        w1_raw[b, a, first // loaded][:, :, local : local + width].rearrange(
                            "p j (m t) -> p m j t", t=PACK
                        ),
                    )
                first = first + width

        def quantise_w1(b, a, widths):
            w1_q[b, a] = quantise("w1q%d%d" % (b, a), w1_grouped[b, a], widths)

        gather_words(0, 1)
        round_w1(0, 0)
        quantise_w1(0, 0, (PASS,))
        gather_words(1, 1)
        round_w1(0, 1)
        quantise_w1(0, 1, (P, 3 * P))

        h_sb = {}

        h_banks = {}

        def h_pass(b, i, s, step):
            a = 1 - step if (b, i) == (0, 2) else step
            codes, plane = w1_q[b, a]
            cols = slice(BANK * s, BANK * (s + 1))
            nc.tensor.matmul_mx(
                out=h_banks[b, i, s][:],
                lhsT=codes[:, P * i : P * (i + 1)].bitcast(E4M3),
                lhsT_scale=plane[:, P * i : P * (i + 1)],
                rhs=v_codes[a][:, cols].bitcast(E4M3),
                rhs_scale=v_plane[a][4 * a :, cols],
                start=(step == 0),
                stop=(step == 1),
            )

        def open_h(b, i, first_bank):
            for s in range(2):
                h_banks[b, i, s] = bank_tile(first_bank + s, [P, BANK])
                h_pass(b, i, s, 0)

        def make_h(b, i, first_bank):
            h_sb[b, i] = held("h%d%d" % (b, i), [P, S], F32)
            for s in range(2):
                if (b, i, s) not in h_banks:
                    h_banks[b, i, s] = bank_tile(first_bank + s, [P, BANK])
                    h_pass(b, i, s, 0)
                h_pass(b, i, s, 1)
                engine = "vector" if (b, i, s) == (0, 0, 0) else "scalar"
                copy_on(engine, h_sb[b, i][:, BANK * s : BANK * (s + 1)], h_banks[b, i, s][:])

        x_first = {}
        x_pair = {}

        def pick(b, i):
            if b == 0:
                x_first[i] = held("x0%d" % i, [P, M], F32, tag=X_TAGS.get((b, i)))
                target = x_first[i][:]
            else:
                if i % 2 == 0:
                    x_pair[i // 2] = held("x1_%d" % (i // 2), [P, 2, M], F32, tag=(None, "x00")[i // 2])
                target = x_pair[i // 2][:, i % 2, :]
            nc.vector.tensor_tensor(out=target, in0=h_sb[b, i][:].indirect(list2[:]), in1=wgt_sb[:], op=ALU.mult)

        d_sb = [held("d%d" % b, [P, PACK, M], F32) for b in range(2)]

        def target_product(bank, b, i, cols):
            rows = slice(PASS * b + P * i, PASS * b + P * (i + 1))
            nc.tensor.matmul_mx(
                out=bank,
                lhsT=wt_codes[:, rows].bitcast(E2M1),
                lhsT_scale=wt_scale[:, rows],
                rhs=tgt_codes[:, cols].bitcast(E4M3),
                rhs_scale=tgt_plane[:, cols],
                start=True,
                stop=True,
            )

        def subtract(i, number):
            bank = bank_tile(number, [P, BANK])
            target_product(bank[:], 0, i, slice(0, M))
            nc.vector.tensor_tensor(out=d_sb[0][:, i, :], in0=bank[:], in1=x_first[i][:], op=ALU.subtract)

        def subtract_pair(pair, u, number):
            cols = slice(half * u, half * (u + 1))
            bank = bank_tile(number, [P, 2, half])
            for n in range(2):
                target_product(bank[:, n, :], 1, 2 * pair + n, cols)
            nc.vector.tensor_tensor(
                out=d_sb[1][:, 2 * pair : 2 * pair + 2, cols], in0=bank[:], in1=x_pair[pair][:, :, cols], op=ALU.subtract
            )

        sq_first = held("sq0", [P, PACK, M], F32, tag="v0")
        e_sb = [held("e%d" % b, [P, PACK, M], F32) for b in range(2)]

        squares = {}

        def square(name, b, first, count, cols):
            if b == 0:
                target = sq_first[:, first : first + count, :]
            else:
                target = held(name, [P, count, cols.stop - cols.start], F32)[:]
            nc.scalar.activation(out=target, in_=d_sb[b][:, first : first + count, cols], func=ACT.Square)
            squares[name] = (target, b, first, count, cols)

        def exponential(name):
            source, b, first, count, cols = squares[name]
            for n in range(count):
                i = first + n
                nc.scalar.activation(
                    out=e_sb[b][:, i, cols], in_=source[:, n, :], func=ACT.Exp, scale=slope_sb[:, b, i : i + 1]
                )

        z_q = {}
        z_sb = {}

        def gain_first(i):
            nc.gpsimd.tensor_scalar(
                out=z_planes[:, i, :],
                in0=e_sb[0][:, i, :],
                scalar1=gain_sb[:, 0, i : i + 1],
                scalar2=0.0,
                op0=ALU.mult,
                op1=ALU.add,
            )

        def weave(u):
            z_sb[0, u] = held("z0_%d" % u, [P, half * PACK], BF16, tag=(None, "sq1_%d" % P)[u])
            nc.vector.tensor_copy(
                out=z_sb[0, u][:].rearrange("p (c i t) -> p c t i", i=4, t=PACK),
                in_=z_planes[:, :, half * u : half * (u + 1)].rearrange("p t (c i) -> p c t i", i=4),
            )

        def quantise_first(u):
            codes = held("z0_codes%d" % u, [P, half], U32, tag="sq1_%d" % (half * u))
            plane = held("z0_plane%d" % u, [P, half], U8)
            quantise_part((codes, plane), z_sb[0, u], 0, half)
            for n in range(2):
                z_q[0, half * u + P * n] = (codes, plane, P * n)

        def quantise_second(m0):
            codes, plane = quantise("z1_%d" % m0, z_sb[1, m0], (P,))
            z_q[1, m0] = (codes, plane, 0)

        def weigh(m0):
            z_sb[1, m0] = held("z1_%d" % m0, [P, P * PACK], BF16)
            nc.vector.tensor_tensor(
                out=z_sb[1, m0][:].rearrange("p (c i t) -> p c t i", i=4, t=PACK),
                in0=e_sb[1][:, :, m0 : m0 + P].rearrange("p t (c i) -> p c t i", i=4),
                in1=gain_sb[:, 1, :].unsqueeze(1).unsqueeze(3).to_broadcast([P, P // 4, PACK, 4]),
                op=ALU.mult,
            )

        out_banks = {}

        def out_passes(m0, turn, b):
            count = N // P // len(OUT_BANKS[m0 // P])
            if b == 0:
                out_banks[m0, turn] = bank_tile(OUT_BANKS[m0 // P][turn], [P, count, P])
            codes, plane, first = z_q[b, m0]
            for n in range(count):
                cols = slice(P * (turn * count + n), P * (turn * count + n + 1))
                nc.tensor.matmul_mx(
                    out=out_banks[m0, turn][:, n, :],
                    lhsT=wo_codes[b][:, cols].bitcast(E4M3),
                    lhsT_scale=wo_plane[:].bitcast(U8)[4 * b :, cols],
                    rhs=codes[:, first : first + P].bitcast(E4M3),
                    rhs_scale=plane[:, first : first + P],
                    start=(b == 0 and n == 0),
                    stop=(b == 1 and n == count - 1),
                )

        def store_out(m0, turn, engine):
            bank = out_banks[m0, turn]
            count, width = N // P // len(OUT_BANKS[m0 // P]), P
            c0 = turn * count
            staged = held("staged%d_%d" % (m0, c0), [P, count, width], F32)
            copy_on(engine, staged[:], bank[:])
            nc.sync.dma_start(
                out=out.rearrange("(c p) m -> p c m", p=P)[:, c0 : c0 + count, m0 : m0 + width], in_=staged[:]
            )

        open_h(0, 0, 0)
        open_h(0, 1, 2)
        make_h(0, 0, 0)
        wt_codes = held("wt_codes", [P, H], U16)
        nc.vector.tensor_copy(
            out=wt_codes[:].rearrange("p (b i m) -> p b i m", b=2, i=PACK),
            in_=wt_raw[:].bitcast(U16).rearrange("p (b m i) -> p b i m", b=2, i=PACK),
        )
        half = M // 2
        tgt_grouped = {}
        tgt_codes = held("tgt_codes", [P, M], U32)
        tgt_plane = held("tgt_plane", [P, M], U8)

        def quantise_tgt(u):
            cols = slice(half * u, half * (u + 1))
            nc.vector.quantize_mx(out=tgt_codes[:, cols].bitcast(E4M3), scales=tgt_plane[:, cols], in_=tgt_grouped[u][:])

        def round_tgt(u, engine, tag):
            tgt_grouped[u] = held("tgt_grouped%d" % u, [P, half * PACK], BF16, tag=tag)
            copy_on(
                engine,
                tgt_grouped[u][:].rearrange("p (c i j) -> p c j i", i=4, j=PACK),
                tgt_raw[u][:].rearrange("p j (c i) -> p c j i", i=4),
            )

        pick(0, 0)
        make_h(0, 1, 2)
        pick(0, 1)
        make_h(0, 2, 4)
        pick(0, 2)
        round_w1(1, 0)
        round_w1(1, 1)
        prepared = [start_quantise("w1q1%d" % a, PASS) for a in range(2)]
        for first, width in ((0, P), (P, 3 * P)):
            for a in (0, 1):
                quantise_part(prepared[a], w1_grouped[1, a], first, width)
        for a in range(2):
            w1_q[1, a] = prepared[a]
        make_h(0, 3, 4)
        round_tgt(0, "scalar", None)
        round_tgt(1, "vector", "h01")
        quantise_tgt(0)
        quantise_tgt(1)
        pick(0, 3)
        make_h(1, 0, 0)
        pick(1, 0)
        make_h(1, 1, 2)
        pick(1, 1)
        make_h(1, 2, 6)
        make_h(1, 3, 4)
        subtract(0, 0)
        subtract(1, 1)
        subtract(2, 2)
        pick(1, 2)
        subtract(3, 3)
        pick(1, 3)
        subtract_pair(0, 0, 6)
        subtract_pair(1, 0, 4)
        subtract_pair(0, 1, 7)
        subtract_pair(1, 1, 5)
        for number in (6, 4, 7, 5, 5):
            target_product(bank_tile(number, [P, BANK])[:], 0, 0, slice(0, M))
        z_planes = held("z_planes", [P, PACK, M], BF16, tag="h12")

        def square_pair(u):
            square("sq1_pair%d" % u, 1, 0, 2, slice(half * u, half * (u + 1)))

        def square_range(m0):
            square("sq1_%d" % m0, 1, 2, 2, slice(m0, m0 + P))

        square("sq0_0", 0, 0, 1, slice(0, M))
        for i in range(PACK):
            if i + 1 < PACK:
                square("sq0_%d" % (i + 1), 0, i + 1, 1, slice(0, M))
            exponential("sq0_%d" % i)
            gain_first(i)
        weave(0)
        square_pair(0)
        square_range(0)
        exponential("sq1_pair0")
        square_range(P)
        exponential("sq1_0")
        square_pair(1)
        exponential("sq1_%d" % P)
        square_range(2 * P)
        exponential("sq1_pair1")
        square_range(3 * P)
        exponential("sq1_%d" % (2 * P))
        exponential("sq1_%d" % (3 * P))
        weigh(0)
        quantise_first(0)
        quantise_second(0)
        for turn in range(2):
            for b in range(2):
                out_passes(0, turn, b)
        for turn in range(2):
            out_passes(P, turn, 0)
        weigh(P)
        weave(1)
        quantise_second(P)
        for turn in range(2):
            out_passes(P, turn, 1)
        store_out(0, 0, "scalar")
        store_out(0, 1, "scalar")
        weigh(2 * P)
        quantise_first(1)
        quantise_second(2 * P)
        for turn in range(2):
            for b in range(2):
                out_passes(2 * P, turn, b)
        for turn in range(3):
            out_passes(3 * P, turn, 0)
        store_out(P, 0, "scalar")
        store_out(P, 1, "scalar")
        weigh(3 * P)
        quantise_second(3 * P)
        for turn in range(3):
            out_passes(3 * P, turn, 1)
        store_out(2 * P, 0, "scalar")
        store_out(2 * P, 1, "vector")
        store_out(3 * P, 0, "scalar")
        store_out(3 * P, 1, "vector")
        store_out(3 * P, 2, "scalar")
